import numpy as np
import ml_dtypes


def mxq(x, axis, fmt="e4m3"):
    dtype, down = {"e4m3": (ml_dtypes.float8_e4m3fn, 7), "e5m2": (ml_dtypes.float8_e5m2, 14)}[fmt]
    v = np.moveaxis(np.asarray(x, np.float32).astype(ml_dtypes.bfloat16).astype(np.float64), axis, -1)
    blocks = v.reshape(v.shape[:-1] + (-1, 32))
    amax = np.abs(blocks).max(-1, keepdims=True)
    byte = np.maximum(np.where(amax > 0, np.frexp(amax)[1] - 1 + 127, 0) - down, 1)
    scale = np.exp2(byte - 127.0)
    codes = (blocks / scale).astype(np.float32).astype(dtype).astype(np.float64)
    return np.moveaxis((codes * scale).reshape(v.shape), -1, axis)


WIDE = False


def mx_kscale(k):
    if not WIDE:
        return np.ones(k)
    levels = np.array([10, -10, 5, -5, 0])
    if k % 512:
        return np.exp2(np.random.permutation(np.resize(levels, k // 32))).repeat(32)
    a = np.empty((k // 512, 16))
    for p in range(k // 512):
        a[p, :8] = np.random.permutation(np.resize(levels, 8))
        for g in range(8):
            far = levels[np.abs(levels - a[p, g]) >= 10]
            a[p, g + 8] = far[np.random.randint(len(far))]
    return np.exp2(a.ravel()).repeat(32)


def f64(x):
    return np.asarray(x).astype(np.float64)


def striped(idx):
    return np.tile(idx.reshape(-1, 16).T, (8, 1)).astype(np.uint16)


def unstriped(offs):
    return offs[:16].T.reshape(-1).astype(np.int64)


E2M1 = np.array([0.0, 0.5, 1.0, 1.5, 2.0, 3.0, 4.0, 6.0, -0.0, -0.5, -1.0, -1.5, -2.0, -3.0, -4.0, -6.0])


def pack_weight(w, fmt):
    k, n = w.shape
    w = f64(np.asarray(w, np.float32).astype(ml_dtypes.bfloat16)).reshape(k // 32, 32, n)
    amax = np.abs(w).max(1)
    if fmt == "e4m3":
        byte = np.frexp(amax)[1] - 1 + 127 - 7
    else:
        mant, ex = np.frexp(amax / 6.0)
        byte = np.where(mant > 0.5, ex, ex - 1) + 127
    byte = np.clip(np.where(amax > 0, byte, 1), 1, 254)
    scaled = (w * np.exp2(127.0 - byte)[:, None, :]).reshape(k, n).astype(np.float32)
    by_word = np.ascontiguousarray(scaled.reshape(k // 512, 128, 4, n).transpose(0, 1, 3, 2))
    if fmt == "e4m3":
        words = by_word.astype(ml_dtypes.float8_e4m3fn).view(np.uint8)
    else:
        c = by_word.astype(ml_dtypes.float4_e2m1fn).view(np.uint8) & 0xF
        words = (c[..., 0::2] | (c[..., 1::2] << 4)).reshape(k // 512, 128, 2 * n)
    return np.ascontiguousarray(words), np.ascontiguousarray(byte.astype(np.uint8).reshape(k // 512, 16, n))


def unpack_weight(words, scales, fmt):
    g, _, n = scales.shape
    words = np.ascontiguousarray(words).reshape(g, 128, n, -1)
    if fmt == "e4m3":
        vals = words.view(ml_dtypes.float8_e4m3fn).astype(np.float64)
    else:
        nib = np.empty((g, 128, n, 4), np.uint8)
        nib[..., 0::2] = words & 0xF
        nib[..., 1::2] = words >> 4
        vals = E2M1[nib]
    vals = vals * np.repeat(np.exp2(scales.astype(np.float64) - 127.0), 8, axis=1)[..., None]
    return vals.transpose(0, 1, 3, 2).reshape(g * 512, n)


K, T, E, C, N = 512, 384, 6, 128, 256


def by_expert(wq, xq):
    return np.concatenate([wq[e].T @ xq[:, e * C:(e + 1) * C] for e in range(E)], axis=1)


def setup_inputs():
    n = np.random.standard_normal
    s = mx_kscale(K)[:, None]
    first = np.random.permutation(np.repeat(np.arange(E), T // E))
    second = (first + 1 + np.random.permutation(np.repeat(np.arange(E - 1), -(-T // (E - 1)))[:T])) % E
    while np.bincount(second, minlength=E).max() != T // E:
        load = np.bincount(second, minlength=E); hi, lo = int(load.argmax()), int(load.argmin())
        t = np.flatnonzero((second == hi) & (first != lo))[0]; second[t] = lo
    slot_token = np.empty(E * C, np.int64); pos = np.empty((2, T), np.int64); fill = np.zeros(E, np.int64)
    place = np.stack([np.random.permutation(C) for _ in range(E)])
    for r, deal in enumerate((first, second)):
        for t in np.random.permutation(T):
            e = deal[t]; j = e * C + place[e, fill[e]]; fill[e] += 1; slot_token[j] = t; pos[r, t] = j
    g = np.random.uniform(0.2, 0.8, T)
    w = [pack_weight(m, "e2m1") for m in n((E + 1, K, N)) / np.sqrt(K) / s[None]]
    return {
        "xT": (n((K, T)) * s).astype(np.float32),
        "w_words": np.stack([m[0] for m in w]),
        "w_scales": np.stack([m[1] for m in w]),
        "b": (0.3 * n((N, E + 1))).astype(np.float32),
        "gate": np.stack([np.tile(g, (N, 1)), np.tile(1.0 - g, (N, 1))]).astype(np.float32),
        "offs": striped(slot_token),
        "pos1": striped(pos[0]),
        "pos2": striped(pos[1]),
    }


def reference(xT, w_words, w_scales, b, gate, offs, pos1, pos2):
    idx = unstriped(offs)
    w = np.stack([unpack_weight(w_words[e], w_scales[e], "e2m1") for e in range(E + 1)])
    wq = w
    xs = mxq(f64(xT), 0, "e4m3")
    ys = (wq[E].T @ xs) + f64(b)[:, E:]
    xq = mxq(f64(xT)[:, idx], 0, "e4m3")
    y = by_expert(w, xq)
    y = y + np.repeat(f64(b)[:, :E], C, axis=1)
    return ys + f64(gate[0]) * y[:, unstriped(pos1)] + f64(gate[1]) * y[:, unstriped(pos2)]

@@ -1,0 +1,209 @@
+from contextlib import ExitStack
+
+import concourse.mybir as mybir
+
+K, T, E, C, N = 512, 384, 6, 128, 256
+S = E * C
+P = 128
+HALVES = N // P
+FLOPS = 2 * K * N * (S + T)
+
+F32 = mybir.dt.float32
+BF16 = mybir.dt.bfloat16
+I32 = mybir.dt.int32
+U32 = mybir.dt.uint32
+U16 = mybir.dt.uint16
+U8 = mybir.dt.uint8
+E4M3X4 = mybir.dt.float8_e4m3fn_x4
+E2M1X4 = mybir.dt.float4_e2m1fn_x4
+
+ADD, MULT = mybir.AluOpType.add, mybir.AluOpType.mult
+COPY, IDENTITY = mybir.ActivationFunctionType.Copy, mybir.ActivationFunctionType.Identity
+
+WINDOW = 1024
+
+
+def tile_moe_shr_lin_bias_kernel(tc, xT, w_words, w_scales, b, gate, offs, pos1, pos2, out):
+    nc = tc.nc
+    with ExitStack() as ctx:
+        lists = ctx.enter_context(tc.tile_pool(name="lists", bufs=1))
+        keep = ctx.enter_context(tc.tile_pool(name="keep", bufs=1))
+        psum = ctx.enter_context(tc.psum_pool(name="psum", bufs=1))
+
+        offs_sb = lists.tile([P, S // 16], U16, name="offs_sb")
+        pos1_sb = lists.tile([P, T // 16], U16, name="pos1_sb")
+        pos2_sb = lists.tile([P, T // 16], U16, name="pos2_sb")
+
+        x_raw = keep.tile([P, 2, 2, T], F32, name="x_raw")
+        pairs = keep.tile([P, 2, WINDOW], U32, name="pairs")
+        slot_x = keep.tile([P, 2 * S], I32, name="slot_x", align_bytes=64)
+        picked = keep.tile([P, 2, S], U32, name="picked")
+        token_x = keep.tile([P, 4 * T], BF16, name="token_x", align_bytes=64)
+        slot_codes = keep.tile([P, S], U32, name="slot_codes", align_bytes=64)
+        slot_scales = keep.tile([P, S], U8, name="slot_scales", align_bytes=64)
+        token_codes = keep.tile([P, T], U32, name="token_codes", align_bytes=64)
+        token_scales = keep.tile([P, T], U8, name="token_scales", align_bytes=64)
+        words = keep.tile([P, E + 1, 2 * N], U8, name="words", align_bytes=64)
+        scales = keep.tile([P, E + 1, N], U8, name="scales", align_bytes=64)
+        bias = keep.tile([P, HALVES, E + 1], F32, name="bias")
+        gates = keep.tile([P, 2, HALVES, T], F32, name="gates")
+        y = [keep.tile([P, S], F32, name=f"y{h}") for h in range(HALVES)]
+        first = [keep.tile([P, T], F32, name=f"first{h}") for h in range(HALVES)]
+        second = [keep.tile([P, T], F32, name=f"second{h}") for h in range(HALVES)]
+        partial = [keep.tile([P, T], F32, name=f"partial{h}") for h in range(HALVES)]
+        result = [keep.tile([P, T], F32, name=f"result{h}") for h in range(HALVES)]
+        warm = keep.tile([P, 2], F32, name="warm")
+        y_ps = [[psum.tile([P, 2 * C], F32, name=f"y_ps{g}_{h}") for h in range(HALVES)] for g in range(E // 2)]
+        ys_ps = [psum.tile([P, T], F32, name=f"ys_ps{h}") for h in range(HALVES)]
+
+        x_view = xT.rearrange("(p u i) t -> p u i t", u=2, i=2)
+        nc.sync.dma_start(out=x_raw[:, 0, :, 0:256], in_=x_view[:, 0, :, 0:256])
+        nc.sync.dma_start(out=x_raw[:, 0, :, 256:T], in_=x_view[:, 0, :, 256:T])
+        nc.sync.dma_start(offs_sb[:], offs)
+        nc.sync.dma_start(out=x_raw[:, 1], in_=x_view[:, 1])
+
+        nc.vector.memset(scales[:].rearrange("p e n -> p (e n)").bitcast(I32), 0)
+        nc.vector.memset(warm[:, 0:1], 0.0)
+        nc.scalar.activation(warm[:, 1:2], warm[:, 0:1], IDENTITY)
+        for u in range(2):
+            nc.gpsimd.memset(pairs[:, u, T:], 0)
+
+        w_scales_i = w_scales.bitcast(I32)
+        for q in range(4):
+            nc.sync.dma_start(
+                out=scales[32 * q : 32 * q + 4].bitcast(I32),
+                in_=w_scales_i[:, 0, 4 * q : 4 * q + 4, :].rearrange("e q n -> q e n"),
+            )
+        nc.sync.dma_start(out=words[:].bitcast(I32), in_=w_words.bitcast(I32).rearrange("e a p x -> p (e a) x"))
+        nc.sync.dma_start(out=bias[:], in_=b.rearrange("(h p) e -> p h e", p=P))
+        nc.sync.dma_start(pos1_sb[:], pos1)
+        nc.sync.dma_start(pos2_sb[:], pos2)
+        nc.sync.dma_start(out=gates[:], in_=gate.rearrange("g (h p) t -> p g h t", p=P))
+
+        def round_pairs(engine_copy, u, lo, hi):
+            engine_copy(
+                pairs[:, u, lo:hi].bitcast(BF16).rearrange("p (t i) -> p t i", i=2),
+                x_raw[:, u, :, lo:hi].rearrange("p i t -> p t i"),
+            )
+
+        def gather(u, lo, hi):
+            nc.vector.tensor_copy(picked[:, u, lo:hi], pairs[:, u, :].indirect(offs_sb[:, lo // 16 : hi // 16]))
+
+        def interleave(lo, hi):
+            nc.vector.tensor_copy(
+                slot_x[:, 2 * lo : 2 * hi].rearrange("p (s u) -> p s u", u=2),
+                picked[:, :, lo:hi].bitcast(I32).rearrange("p u s -> p s u"),
+            )
+
+        def interleave_on_scalar(lo, hi):
+            nc.scalar.copy(
+                slot_x[:, 2 * lo : 2 * hi].bitcast(BF16).rearrange("p (s u i) -> p s u i", u=2, i=2),
+                picked[:, :, lo:hi].bitcast(BF16).rearrange("p u (s i) -> p s u i", i=2),
+            )
+
+        def quantize_slots(lo, hi):
+            nc.vector.quantize_mx(
+                out=slot_codes[:, lo:hi].bitcast(E4M3X4),
+                scales=slot_scales[:, lo:hi],
+                in_=slot_x[:, 2 * lo : 2 * hi].bitcast(BF16),
+            )
+
+        def quantize_tokens(lo, hi):
+            nc.vector.quantize_mx(
+                out=token_codes[:, lo:hi].bitcast(E4M3X4),
+                scales=token_scales[:, lo:hi],
+                in_=token_x[:, 4 * lo : 4 * hi],
+            )
+
+        def multiply(acc, e, h, codes, code_scales):
+            nc.tensor.matmul_mx(
+                out=acc,
+                lhsT=words[:, e, 2 * P * h : 2 * P * (h + 1)].bitcast(E2M1X4),
+                lhsT_scale=scales[:, e, P * h : P * (h + 1)],
+                rhs=codes.bitcast(E4M3X4),
+                rhs_scale=code_scales,
+                start=True,
+                stop=True,
+            )
+
+        def products(experts):
+            for h in range(HALVES):
+                for e in experts:
+                    product(e, h)
+
+        def product(e, h):
+            lo, hi = e * C, (e + 1) * C
+            multiply(y_ps[e // 2][h][:, (e % 2) * C : (e % 2 + 1) * C], e, h, slot_codes[:, lo:hi], slot_scales[:, lo:hi])
+
+        def empty(e, h):
+            nc.scalar.activation(
+                y[h][:, e * C : (e + 1) * C],
+                y_ps[e // 2][h][:, (e % 2) * C : (e % 2 + 1) * C],
+                IDENTITY,
+                bias=bias[:, h, e : e + 1],
+            )
+
+        def shared(lo, hi):
+            for h in range(HALVES):
+                multiply(ys_ps[h][:, lo:hi], E, h, token_codes[:, lo:hi], token_scales[:, lo:hi])
+
+        round_pairs(nc.vector.tensor_copy, 0, 0, 256)
+        round_pairs(nc.vector.tensor_copy, 0, 256, T)
+        round_pairs(nc.scalar.copy, 1, 0, T)
+        nc.scalar.copy(
+            token_x[:].rearrange("p (t u i) -> p t u i", u=2, i=2),
+            pairs[:, :, 0:T].bitcast(BF16).rearrange("p u (t i) -> p t u i", i=2),
+        )
+
+        gather(0, 0, S)
+        gather(1, 0, 256)
+        gather(1, 256, 512)
+        interleave_on_scalar(256, 512)
+        interleave(0, 256)
+        gather(1, 512, 768)
+        quantize_slots(0, 256)
+        products((0, 1))
+        for h in range(HALVES):
+            for e in (0, 1):
+                empty(e, h)
+        interleave(512, 768)
+        quantize_slots(256, 512)
+        products((2, 3))
+        empty(2, 0)
+        empty(3, 0)
+        quantize_slots(512, 768)
+        products((4, 5))
+        empty(4, 0)
+        empty(5, 0)
+        for e in range(2, E):
+            empty(e, 1)
+        quantize_tokens(256, 384)
+        quantize_tokens(0, 256)
+        shared(256, 384)
+        shared(0, 256)
+
+        def fetch(dst, h, g, lo, hi):
+            nc.vector.tensor_tensor(
+                dst[:, lo:hi],
+                y[h][:].indirect((pos1_sb, pos2_sb)[g][:, lo // 16 : hi // 16]),
+                gates[:, g, h, lo:hi],
+                MULT,
+            )
+
+        def add_shared(h):
+            nc.vector.scalar_tensor_tensor(partial[h][:], ys_ps[h][:], bias[:, h, E : E + 1], first[h][:], ADD, ADD)
+
+        def finish(h, lo, hi):
+            nc.vector.tensor_tensor(result[h][:, lo:hi], partial[h][:, lo:hi], second[h][:, lo:hi], ADD)
+            nc.sync.dma_start(out=out[h * P : (h + 1) * P, lo:hi], in_=result[h][:, lo:hi])
+
+        fetch(first[0], 0, 0, 0, T)
+        fetch(second[0], 0, 1, 0, T)
+        add_shared(0)
+        fetch(first[1], 1, 0, 0, T)
+        finish(0, 0, T)
+        fetch(second[1], 1, 1, 0, 256)
+        add_shared(1)
+        fetch(second[1], 1, 1, 256, T)
+        finish(1, 0, 256)
+        finish(1, 256, T)

@@ -21,6 +21,7 @@ ADD, MULT = mybir.AluOpType.add, mybir.AluOpType.mult
 COPY, IDENTITY = mybir.ActivationFunctionType.Copy, mybir.ActivationFunctionType.Identity
 
 WINDOW = 1024
+PIECES = ((0, 256), (256, 512), (512, 640), (640, 768))
 
 
 def tile_moe_shr_lin_bias_kernel(tc, xT, w_words, w_scales, b, gate, offs, pos1, pos2, out):
@@ -36,25 +37,31 @@ def tile_moe_shr_lin_bias_kernel(tc, xT, w_words, w_scales, b, gate, offs, pos1,
 
         x_raw = keep.tile([P, 2, 2, T], F32, name="x_raw")
         pairs = keep.tile([P, 2, WINDOW], U32, name="pairs")
-        slot_x = keep.tile([P, 2 * S], I32, name="slot_x", align_bytes=64)
-        picked = keep.tile([P, 2, S], U32, name="picked")
-        token_x = keep.tile([P, 4 * T], BF16, name="token_x", align_bytes=64)
+        picked = [
+            keep.tile([P, 2 * (hi - lo)], U32, name=f"picked{j}", tag=f"picked{j}", align_bytes=64)
+            for j, (lo, hi) in enumerate(PIECES[:-1])
+        ]
+        slot_x = [
+            keep.tile([P, 2 * (hi - lo)], U32, name=f"slot_x{j}", align_bytes=64) for j, (lo, hi) in enumerate(PIECES[:-1])
+        ]
+        token_x = keep.tile([P, 2 * T], U32, name="token_x", align_bytes=64)
         slot_codes = keep.tile([P, S], U32, name="slot_codes", align_bytes=64)
         slot_scales = keep.tile([P, S], U8, name="slot_scales", align_bytes=64)
-        token_codes = keep.tile([P, T], U32, name="token_codes", align_bytes=64)
         token_scales = keep.tile([P, T], U8, name="token_scales", align_bytes=64)
         words = keep.tile([P, E + 1, 2 * N], U8, name="words", align_bytes=64)
         scales = keep.tile([P, E + 1, N], U8, name="scales", align_bytes=64)
         bias = keep.tile([P, HALVES, E + 1], F32, name="bias")
-        gates = keep.tile([P, 2, HALVES, T], F32, name="gates")
+        gates = keep.tile([P, 2, T], F32, name="gates")
         y = [keep.tile([P, S], F32, name=f"y{h}") for h in range(HALVES)]
         first = [keep.tile([P, T], F32, name=f"first{h}") for h in range(HALVES)]
         second = [keep.tile([P, T], F32, name=f"second{h}") for h in range(HALVES)]
         partial = [keep.tile([P, T], F32, name=f"partial{h}") for h in range(HALVES)]
         result = [keep.tile([P, T], F32, name=f"result{h}") for h in range(HALVES)]
         warm = keep.tile([P, 2], F32, name="warm")
-        y_ps = [[psum.tile([P, 2 * C], F32, name=f"y_ps{g}_{h}") for h in range(HALVES)] for g in range(E // 2)]
-        ys_ps = [psum.tile([P, T], F32, name=f"ys_ps{h}") for h in range(HALVES)]
+        y_ps = [
+            [psum.tile([P, 2 * C], F32, name=f"y_ps{h}_{j}", tag=f"bank{h}_{j}") for j in range(len(PIECES) - h)]
+            for h in range(HALVES)
+        ]
 
         x_view = xT.rearrange("(p u i) t -> p u i t", u=2, i=2)
         nc.sync.dma_start(out=x_raw[:, 0, :, 0:256], in_=x_view[:, 0, :, 0:256])
@@ -78,7 +85,7 @@ def tile_moe_shr_lin_bias_kernel(tc, xT, w_words, w_scales, b, gate, offs, pos1,
         nc.sync.dma_start(out=bias[:], in_=b.rearrange("(h p) e -> p h e", p=P))
         nc.sync.dma_start(pos1_sb[:], pos1)
         nc.sync.dma_start(pos2_sb[:], pos2)
-        nc.sync.dma_start(out=gates[:], in_=gate.rearrange("g (h p) t -> p g h t", p=P))
+        nc.sync.dma_start(out=gates[:], in_=gate[:, 0:P, :].rearrange("g p t -> p g t"))
 
         def round_pairs(engine_copy, u, lo, hi):
             engine_copy(
@@ -86,33 +93,29 @@ def tile_moe_shr_lin_bias_kernel(tc, xT, w_words, w_scales, b, gate, offs, pos1,
                 x_raw[:, u, :, lo:hi].rearrange("p i t -> p t i"),
             )
 
-        def gather(u, lo, hi):
-            nc.vector.tensor_copy(picked[:, u, lo:hi], pairs[:, u, :].indirect(offs_sb[:, lo // 16 : hi // 16]))
+        def gather(u, j):
+            lo, hi = PIECES[j]
+            n = hi - lo
+            nc.vector.tensor_copy(picked[j][:, u * n : (u + 1) * n], pairs[:, u, :].indirect(offs_sb[:, lo // 16 : hi // 16]))
 
-        def interleave(lo, hi):
+        def gather_woven(dst, u, j):
+            lo, hi = PIECES[j]
             nc.vector.tensor_copy(
-                slot_x[:, 2 * lo : 2 * hi].rearrange("p (s u) -> p s u", u=2),
-                picked[:, :, lo:hi].bitcast(I32).rearrange("p u s -> p s u"),
+                dst[:].rearrange("p (s u) -> p u s", u=2)[:, u, :], pairs[:, u, :].indirect(offs_sb[:, lo // 16 : hi // 16])
             )
 
-        def interleave_on_scalar(lo, hi):
-            nc.scalar.copy(
-                slot_x[:, 2 * lo : 2 * hi].bitcast(BF16).rearrange("p (s u i) -> p s u i", u=2, i=2),
-                picked[:, :, lo:hi].bitcast(BF16).rearrange("p u (s i) -> p s u i", i=2),
-            )
+        def interleave(j):
+            nc.scalar.copy(slot_x[j][:].rearrange("p (s u) -> p s u", u=2), picked[j][:].rearrange("p (u s) -> p s u", u=2))
 
-        def quantize_slots(lo, hi):
-            nc.vector.quantize_mx(
-                out=slot_codes[:, lo:hi].bitcast(E4M3X4),
-                scales=slot_scales[:, lo:hi],
-                in_=slot_x[:, 2 * lo : 2 * hi].bitcast(BF16),
-            )
+        def quantize_slots(src, j):
+            lo, hi = PIECES[j]
+            nc.vector.quantize_mx(out=slot_codes[:, lo:hi].bitcast(E4M3X4), scales=slot_scales[:, lo:hi], in_=src[:].bitcast(BF16))
 
         def quantize_tokens(lo, hi):
             nc.vector.quantize_mx(
                 out=token_codes[:, lo:hi].bitcast(E4M3X4),
                 scales=token_scales[:, lo:hi],
-                in_=token_x[:, 4 * lo : 4 * hi],
+                in_=token_x[:, 2 * lo : 2 * hi].bitcast(BF16),
             )
 
         def multiply(acc, e, h, codes, code_scales):
@@ -126,22 +129,22 @@ def tile_moe_shr_lin_bias_kernel(tc, xT, w_words, w_scales, b, gate, offs, pos1,
                 stop=True,
             )
 
-        def products(experts):
-            for h in range(HALVES):
-                for e in experts:
-                    product(e, h)
+        def place(e, h):
+            j = [lo <= e * C < hi for lo, hi in PIECES].index(True)
+            j = min(j, len(y_ps[h]) - 1)
+            at = e * C - PIECES[j][0]
+            return y_ps[h][j][:, at : at + C]
 
-        def product(e, h):
-            lo, hi = e * C, (e + 1) * C
-            multiply(y_ps[e // 2][h][:, (e % 2) * C : (e % 2 + 1) * C], e, h, slot_codes[:, lo:hi], slot_scales[:, lo:hi])
+        def experts_of(j):
+            return range(PIECES[j][0] // C, PIECES[j][1] // C)
 
-        def empty(e, h):
-            nc.scalar.activation(
-                y[h][:, e * C : (e + 1) * C],
-                y_ps[e // 2][h][:, (e % 2) * C : (e % 2 + 1) * C],
-                IDENTITY,
-                bias=bias[:, h, e : e + 1],
-            )
+        def products(j, h):
+            for e in experts_of(j):
+                multiply(place(e, h), e, h, slot_codes[:, e * C : (e + 1) * C], slot_scales[:, e * C : (e + 1) * C])
+
+        def empty(j, h):
+            for e in experts_of(j):
+                nc.scalar.activation(y[h][:, e * C : (e + 1) * C], place(e, h), IDENTITY, bias=bias[:, h, e : e + 1])
 
         def shared(lo, hi):
             for h in range(HALVES):
@@ -150,33 +153,29 @@ def tile_moe_shr_lin_bias_kernel(tc, xT, w_words, w_scales, b, gate, offs, pos1,
         round_pairs(nc.vector.tensor_copy, 0, 0, 256)
         round_pairs(nc.vector.tensor_copy, 0, 256, T)
         round_pairs(nc.scalar.copy, 1, 0, T)
-        nc.scalar.copy(
-            token_x[:].rearrange("p (t u i) -> p t u i", u=2, i=2),
-            pairs[:, :, 0:T].bitcast(BF16).rearrange("p u (t i) -> p t u i", i=2),
-        )
+        nc.scalar.copy(token_x[:].rearrange("p (t u) -> p t u", u=2), pairs[:, :, 0:T].rearrange("p u t -> p t u"))
 
-        gather(0, 0, S)
-        gather(1, 0, 256)
-        gather(1, 256, 512)
-        interleave_on_scalar(256, 512)
-        interleave(0, 256)
-        gather(1, 512, 768)
-        quantize_slots(0, 256)
-        products((0, 1))
-        for h in range(HALVES):
-            for e in (0, 1):
-                empty(e, h)
-        interleave(512, 768)
-        quantize_slots(256, 512)
-        products((2, 3))
-        empty(2, 0)
-        empty(3, 0)
-        quantize_slots(512, 768)
-        products((4, 5))
-        empty(4, 0)
-        empty(5, 0)
-        for e in range(2, E):
-            empty(e, 1)
+        for u in range(2):
+            for j in range(3):
+                gather(u, j)
+        for j in range(3):
+            interleave(j)
+        quantize_slots(slot_x[0], 0)
+        products(0, 0)
+        empty(0, 0)
+        woven = keep.tile([P, 2 * C], U32, name="woven", tag="picked0", align_bytes=64)
+        for u in range(2):
+            gather_woven(woven, u, 3)
+        for j in (1, 2, 3):
+            quantize_slots(slot_x[j] if j < 3 else woven, j)
+            products(j, 0)
+            empty(j, 0)
+        for j in range(4):
+            products(j, 1)
+        for j in range(4):
+            empty(j, 1)
+        token_codes = keep.tile([P, T], U32, name="token_codes", tag="picked2", align_bytes=64)
+        ys_ps = [psum.tile([P, T], F32, name=f"ys_ps{h}", tag=f"bank0_{h}") for h in range(HALVES)]
         quantize_tokens(256, 384)
         quantize_tokens(0, 256)
         shared(256, 384)
@@ -186,7 +185,7 @@ def tile_moe_shr_lin_bias_kernel(tc, xT, w_words, w_scales, b, gate, offs, pos1,
             nc.vector.tensor_tensor(
                 dst[:, lo:hi],
                 y[h][:].indirect((pos1_sb, pos2_sb)[g][:, lo // 16 : hi // 16]),
-                gates[:, g, h, lo:hi],
+                gates[:, g, lo:hi],
                 MULT,
             )
 

@@ -1,6 +1,7 @@
 from contextlib import ExitStack
 
 import concourse.mybir as mybir
+from concourse.masks import make_identity
 
 K, T, E, C, N = 512, 384, 6, 128, 256
 S = E * C
@@ -20,7 +21,7 @@ E2M1X4 = mybir.dt.float4_e2m1fn_x4
 ADD, MULT = mybir.AluOpType.add, mybir.AluOpType.mult
 COPY, IDENTITY = mybir.ActivationFunctionType.Copy, mybir.ActivationFunctionType.Identity
 
-WINDOW = 1024
+WINDOW = 512
 PIECES = ((0, 256), (256, 512), (512, 640), (640, 768))
 
 
@@ -55,7 +56,10 @@ def tile_moe_shr_lin_bias_kernel(tc, xT, w_words, w_scales, b, gate, offs, pos1,
         y = [keep.tile([P, S], F32, name=f"y{h}") for h in range(HALVES)]
         first = [keep.tile([P, T], F32, name=f"first{h}") for h in range(HALVES)]
         second = [keep.tile([P, T], F32, name=f"second{h}") for h in range(HALVES)]
-        partial = [keep.tile([P, T], F32, name=f"partial{h}") for h in range(HALVES)]
+        base = keep.tile([P, T], F32, name="base")
+        turned = keep.tile([P, T], F32, name="turned")
+        partial = keep.tile([P, T], F32, name="partial")
+        identity = keep.tile([P, P], F32, name="identity")
         result = [keep.tile([P, T], F32, name=f"result{h}") for h in range(HALVES)]
         warm = keep.tile([P, 2], F32, name="warm")
         y_ps = [
@@ -74,6 +78,7 @@ def tile_moe_shr_lin_bias_kernel(tc, xT, w_words, w_scales, b, gate, offs, pos1,
         nc.scalar.activation(warm[:, 1:2], warm[:, 0:1], IDENTITY)
         for u in range(2):
             nc.gpsimd.memset(pairs[:, u, T:], 0)
+        make_identity(nc, identity[:])
 
         w_scales_i = w_scales.bitcast(I32)
         for q in range(4):
@@ -146,8 +151,8 @@ def tile_moe_shr_lin_bias_kernel(tc, xT, w_words, w_scales, b, gate, offs, pos1,
             for e in experts_of(j):
                 nc.scalar.activation(y[h][:, e * C : (e + 1) * C], place(e, h), IDENTITY, bias=bias[:, h, e : e + 1])
 
-        def shared(lo, hi):
-            for h in range(HALVES):
+        def shared(h):
+            for lo, hi in ((256, T), (0, 256)):
                 multiply(ys_ps[h][:, lo:hi], E, h, token_codes[:, lo:hi], token_scales[:, lo:hi])
 
         round_pairs(nc.vector.tensor_copy, 0, 0, 256)
@@ -170,16 +175,17 @@ def tile_moe_shr_lin_bias_kernel(tc, xT, w_words, w_scales, b, gate, offs, pos1,
             quantize_slots(slot_x[j] if j < 3 else woven, j)
             products(j, 0)
             empty(j, 0)
+        token_codes = keep.tile([P, T], U32, name="token_codes", tag="picked2", align_bytes=64)
+        ys_ps = [psum.tile([P, T], F32, name=f"ys_ps{h}", tag=("spare", "bank0_1")[h]) for h in range(HALVES)]
+        quantize_tokens(256, 384)
+        quantize_tokens(0, 256)
+        shared(0)
+        nc.scalar.activation(base[:], ys_ps[0][:], IDENTITY, bias=bias[:, 0, E : E + 1])
         for j in range(4):
             products(j, 1)
         for j in range(4):
             empty(j, 1)
-        token_codes = keep.tile([P, T], U32, name="token_codes", tag="picked2", align_bytes=64)
-        ys_ps = [psum.tile([P, T], F32, name=f"ys_ps{h}", tag=f"bank0_{h}") for h in range(HALVES)]
-        quantize_tokens(256, 384)
-        quantize_tokens(0, 256)
-        shared(256, 384)
-        shared(0, 256)
+        shared(1)
 
         def fetch(dst, h, g, lo, hi):
             nc.vector.tensor_tensor(
@@ -189,20 +195,34 @@ def tile_moe_shr_lin_bias_kernel(tc, xT, w_words, w_scales, b, gate, offs, pos1,
                 MULT,
             )
 
-        def add_shared(h):
-            nc.vector.scalar_tensor_tensor(partial[h][:], ys_ps[h][:], bias[:, h, E : E + 1], first[h][:], ADD, ADD)
+        def turn(dst, src, start, stop):
+            nc.tensor.matmul(dst, lhsT=src, rhs=identity[:], is_transpose=True, start=start, stop=stop)
 
-        def finish(h, lo, hi):
-            nc.vector.tensor_tensor(result[h][:, lo:hi], partial[h][:, lo:hi], second[h][:, lo:hi], ADD)
-            nc.sync.dma_start(out=out[h * P : (h + 1) * P, lo:hi], in_=result[h][:, lo:hi])
+        def block(j):
+            return slice(j * P, (j + 1) * P)
+
+        sums = [psum.tile([P, P], F32, name=f"sum{j}", tag=("bank0_0", "bank0_2", "bank0_3")[j]) for j in range(3)]
+        back = [psum.tile([P, hi - lo], F32, name=f"back{lo}", tag=tag) for lo, hi, tag in ((0, 256, "spare"), (256, T, "bank1_0"))]
 
         fetch(first[0], 0, 0, 0, T)
-        fetch(second[0], 0, 1, 0, T)
-        add_shared(0)
+        for j in range(3):
+            turn(sums[j][:], first[0][:, block(j)], True, False)
+            turn(sums[j][:], base[:, block(j)], False, False)
+        fetch(second[0], 0, 1, 0, 256)
+        fetch(second[0], 0, 1, 256, T)
+        for j in range(3):
+            turn(sums[j][:], second[0][:, block(j)], False, True)
+        for j in range(3):
+            nc.scalar.copy(turned[:, block(j)], sums[j][:])
+        for j in range(3):
+            turn(back[j // 2][:, block(j % 2)], turned[:, block(j)], True, True)
+        nc.scalar.copy(result[0][:, 0:256], back[0][:])
+        nc.scalar.copy(result[0][:, 256:T], back[1][:])
+        nc.scalar.dma_start(out=out[0:P, :], in_=result[0][:])
         fetch(first[1], 1, 0, 0, T)
-        finish(0, 0, T)
         fetch(second[1], 1, 1, 0, 256)
-        add_shared(1)
+        nc.vector.scalar_tensor_tensor(partial[:], ys_ps[1][:], bias[:, 1, E : E + 1], first[1][:], ADD, ADD)
         fetch(second[1], 1, 1, 256, T)
-        finish(1, 0, 256)
-        finish(1, 256, T)
+        for lo, hi, queue in ((0, 256, nc.sync), (256, T, nc.sync)):
+            nc.vector.tensor_tensor(result[1][:, lo:hi], partial[:, lo:hi], second[1][:, lo:hi], ADD)
+            queue.dma_start(out=out[P : 2 * P, lo:hi], in_=result[1][:, lo:hi])

@@ -40,18 +40,16 @@ def tile_moe_shr_lin_bias_kernel(tc, xT, w_words, w_scales, b, gate, offs, pos1,
         pairs = keep.tile([P, 2, WINDOW], U32, name="pairs")
         picked = [
             keep.tile([P, 2 * (hi - lo)], U32, name=f"picked{j}", tag=f"picked{j}", align_bytes=64)
-            for j, (lo, hi) in enumerate(PIECES[:-1])
+            for j, (lo, hi) in enumerate(PIECES)
         ]
-        slot_x = [
-            keep.tile([P, 2 * (hi - lo)], U32, name=f"slot_x{j}", align_bytes=64) for j, (lo, hi) in enumerate(PIECES[:-1])
-        ]
+        slot_x = [keep.tile([P, 2 * (hi - lo)], U32, name=f"slot_x{j}", align_bytes=64) for j, (lo, hi) in enumerate(PIECES)]
         token_x = keep.tile([P, 2 * T], U32, name="token_x", align_bytes=64)
         slot_codes = keep.tile([P, S], U32, name="slot_codes", align_bytes=64)
         slot_scales = keep.tile([P, S], U8, name="slot_scales", align_bytes=64)
         token_scales = keep.tile([P, T], U8, name="token_scales", align_bytes=64)
         words = keep.tile([P, E + 1, 2 * N], U8, name="words", align_bytes=64)
         scales = keep.tile([P, E + 1, N], U8, name="scales", align_bytes=64)
-        bias = keep.tile([P, HALVES, E + 1], F32, name="bias")
+        bias = keep.tile([P, HALVES, 8], F32, name="bias")
         gates = keep.tile([P, 2, T], F32, name="gates")
         y = [keep.tile([P, S], F32, name=f"y{h}") for h in range(HALVES)]
         first = [keep.tile([P, T], F32, name=f"first{h}") for h in range(HALVES)]
@@ -62,10 +60,7 @@ def tile_moe_shr_lin_bias_kernel(tc, xT, w_words, w_scales, b, gate, offs, pos1,
         identity = keep.tile([P, P], F32, name="identity")
         result = [keep.tile([P, T], F32, name=f"result{h}") for h in range(HALVES)]
         warm = keep.tile([P, 2], F32, name="warm")
-        y_ps = [
-            [psum.tile([P, 2 * C], F32, name=f"y_ps{h}_{j}", tag=f"bank{h}_{j}") for j in range(len(PIECES) - h)]
-            for h in range(HALVES)
-        ]
+        y_ps = [[psum.tile([P, 2 * C], F32, name=f"y_ps0_{j}", tag=f"bank0_{j}") for j in range(len(PIECES))]]
 
         x_view = xT.rearrange("(p u i) t -> p u i t", u=2, i=2)
         nc.sync.dma_start(out=x_raw[:, 0, :, 0:256], in_=x_view[:, 0, :, 0:256])
@@ -87,7 +82,7 @@ def tile_moe_shr_lin_bias_kernel(tc, xT, w_words, w_scales, b, gate, offs, pos1,
                 in_=w_scales_i[:, 0, 4 * q : 4 * q + 4, :].rearrange("e q n -> q e n"),
             )
         nc.sync.dma_start(out=words[:].bitcast(I32), in_=w_words.bitcast(I32).rearrange("e a p x -> p (e a) x"))
-        nc.sync.dma_start(out=bias[:], in_=b.rearrange("(h p) e -> p h e", p=P))
+        nc.sync.dma_start(out=bias[:, :, 0 : E + 1], in_=b.rearrange("(h p) e -> p h e", p=P))
         nc.sync.dma_start(pos1_sb[:], pos1)
         nc.sync.dma_start(pos2_sb[:], pos2)
         nc.sync.dma_start(out=gates[:], in_=gate[:, 0:P, :].rearrange("g p t -> p g t"))
@@ -102,12 +97,6 @@ def tile_moe_shr_lin_bias_kernel(tc, xT, w_words, w_scales, b, gate, offs, pos1,
             lo, hi = PIECES[j]
             n = hi - lo
             nc.vector.tensor_copy(picked[j][:, u * n : (u + 1) * n], pairs[:, u, :].indirect(offs_sb[:, lo // 16 : hi // 16]))
-
-        def gather_woven(dst, u, j):
-            lo, hi = PIECES[j]
-            nc.vector.tensor_copy(
-                dst[:].rearrange("p (s u) -> p u s", u=2)[:, u, :], pairs[:, u, :].indirect(offs_sb[:, lo // 16 : hi // 16])
-            )
 
         def interleave(j):
             nc.scalar.copy(slot_x[j][:].rearrange("p (s u) -> p s u", u=2), picked[j][:].rearrange("p (u s) -> p s u", u=2))
@@ -161,26 +150,26 @@ def tile_moe_shr_lin_bias_kernel(tc, xT, w_words, w_scales, b, gate, offs, pos1,
         nc.scalar.copy(token_x[:].rearrange("p (t u) -> p t u", u=2), pairs[:, :, 0:T].rearrange("p u t -> p t u"))
 
         for u in range(2):
-            for j in range(3):
+            for j in range(4):
                 gather(u, j)
-        for j in range(3):
+        for j in range(4):
             interleave(j)
         quantize_slots(slot_x[0], 0)
         products(0, 0)
         empty(0, 0)
-        woven = keep.tile([P, 2 * C], U32, name="woven", tag="picked0", align_bytes=64)
-        for u in range(2):
-            gather_woven(woven, u, 3)
         for j in (1, 2, 3):
-            quantize_slots(slot_x[j] if j < 3 else woven, j)
+            quantize_slots(slot_x[j], j)
             products(j, 0)
-            empty(j, 0)
-        token_codes = keep.tile([P, T], U32, name="token_codes", tag="picked2", align_bytes=64)
-        ys_ps = [psum.tile([P, T], F32, name=f"ys_ps{h}", tag=("spare", "bank0_1")[h]) for h in range(HALVES)]
+        empty(1, 0)
+        for e in (E - 2, E - 1):
+            nc.vector.tensor_scalar_add(y[0][:, e * C : (e + 1) * C], place(e, 0), bias[:, 0, e : e + 1])
+        token_codes = keep.tile([P, T], U32, name="token_codes", tag="picked3", align_bytes=64)
+        ys_ps = [psum.tile([P, T], F32, name=f"ys_ps{h}", tag=("spare", "bank0_2")[h]) for h in range(HALVES)]
         quantize_tokens(256, 384)
         quantize_tokens(0, 256)
         shared(0)
         nc.scalar.activation(base[:], ys_ps[0][:], IDENTITY, bias=bias[:, 0, E : E + 1])
+        y_ps.append([psum.tile([P, 2 * C], F32, name=f"y_ps1_{j}", tag=("bank0_1", "bank0_0", "bank1_0")[j]) for j in range(3)])
         for j in range(4):
             products(j, 1)
         for j in range(4):
@@ -201,7 +190,7 @@ def tile_moe_shr_lin_bias_kernel(tc, xT, w_words, w_scales, b, gate, offs, pos1,
         def block(j):
             return slice(j * P, (j + 1) * P)
 
-        sums = [psum.tile([P, P], F32, name=f"sum{j}", tag=("bank0_0", "bank0_2", "bank0_3")[j]) for j in range(3)]
+        sums = [psum.tile([P, P], F32, name=f"sum{j}", tag=("bank1_1", "bank1_2", "bank0_3")[j]) for j in range(3)]
         back = [psum.tile([P, hi - lo], F32, name=f"back{lo}", tag=tag) for lo, hi, tag in ((0, 256, "spare"), (256, T, "bank1_0"))]
 
         fetch(first[0], 0, 0, 0, T)

@@ -21,7 +21,7 @@ E2M1X4 = mybir.dt.float4_e2m1fn_x4
 ADD, MULT = mybir.AluOpType.add, mybir.AluOpType.mult
 COPY, IDENTITY = mybir.ActivationFunctionType.Copy, mybir.ActivationFunctionType.Identity
 
-WINDOW = 512
+WINDOWS = (1024, 512)
 PIECES = ((0, 256), (256, 512), (512, 640), (640, 768))
 
 
@@ -37,11 +37,8 @@ def tile_moe_shr_lin_bias_kernel(tc, xT, w_words, w_scales, b, gate, offs, pos1,
         pos2_sb = lists.tile([P, T // 16], U16, name="pos2_sb")
 
         x_raw = keep.tile([P, 2, 2, T], F32, name="x_raw")
-        pairs = keep.tile([P, 2, WINDOW], U32, name="pairs")
-        picked = [
-            keep.tile([P, 2 * (hi - lo)], U32, name=f"picked{j}", tag=f"picked{j}", align_bytes=64)
-            for j, (lo, hi) in enumerate(PIECES)
-        ]
+        pairs = keep.tile([P, 2, WINDOWS[0]], U32, name="pairs")
+        picked = keep.tile([P, 2, S], U32, name="picked", tag="picked", align_bytes=64)
         slot_x = [keep.tile([P, 2 * (hi - lo)], U32, name=f"slot_x{j}", align_bytes=64) for j, (lo, hi) in enumerate(PIECES)]
         token_x = keep.tile([P, 2 * T], U32, name="token_x", align_bytes=64)
         slot_codes = keep.tile([P, S], U32, name="slot_codes", align_bytes=64)
@@ -63,8 +60,7 @@ def tile_moe_shr_lin_bias_kernel(tc, xT, w_words, w_scales, b, gate, offs, pos1,
         y_ps = [[psum.tile([P, 2 * C], F32, name=f"y_ps0_{j}", tag=f"bank0_{j}") for j in range(len(PIECES))]]
 
         x_view = xT.rearrange("(p u i) t -> p u i t", u=2, i=2)
-        nc.sync.dma_start(out=x_raw[:, 0, :, 0:256], in_=x_view[:, 0, :, 0:256])
-        nc.sync.dma_start(out=x_raw[:, 0, :, 256:T], in_=x_view[:, 0, :, 256:T])
+        nc.sync.dma_start(out=x_raw[:, 0], in_=x_view[:, 0])
         nc.sync.dma_start(offs_sb[:], offs)
         nc.sync.dma_start(out=x_raw[:, 1], in_=x_view[:, 1])
 
@@ -72,7 +68,7 @@ def tile_moe_shr_lin_bias_kernel(tc, xT, w_words, w_scales, b, gate, offs, pos1,
         nc.vector.memset(warm[:, 0:1], 0.0)
         nc.scalar.activation(warm[:, 1:2], warm[:, 0:1], IDENTITY)
         for u in range(2):
-            nc.gpsimd.memset(pairs[:, u, T:], 0)
+            nc.gpsimd.memset(pairs[:, u, T : WINDOWS[u]], 0)
         make_identity(nc, identity[:])
 
         w_scales_i = w_scales.bitcast(I32)
@@ -93,13 +89,12 @@ def tile_moe_shr_lin_bias_kernel(tc, xT, w_words, w_scales, b, gate, offs, pos1,
                 x_raw[:, u, :, lo:hi].rearrange("p i t -> p t i"),
             )
 
-        def gather(u, j):
-            lo, hi = PIECES[j]
-            n = hi - lo
-            nc.vector.tensor_copy(picked[j][:, u * n : (u + 1) * n], pairs[:, u, :].indirect(offs_sb[:, lo // 16 : hi // 16]))
+        def gather(u, lo, hi):
+            nc.vector.tensor_copy(picked[:, u, lo:hi], pairs[:, u, 0 : WINDOWS[u]].indirect(offs_sb[:, lo // 16 : hi // 16]))
 
         def interleave(j):
-            nc.scalar.copy(slot_x[j][:].rearrange("p (s u) -> p s u", u=2), picked[j][:].rearrange("p (u s) -> p s u", u=2))
+            lo, hi = PIECES[j]
+            nc.scalar.copy(slot_x[j][:].rearrange("p (s u) -> p s u", u=2), picked[:, :, lo:hi].rearrange("p u s -> p s u"))
 
         def quantize_slots(src, j):
             lo, hi = PIECES[j]
@@ -145,13 +140,13 @@ def tile_moe_shr_lin_bias_kernel(tc, xT, w_words, w_scales, b, gate, offs, pos1,
                 multiply(ys_ps[h][:, lo:hi], E, h, token_codes[:, lo:hi], token_scales[:, lo:hi])
 
         round_pairs(nc.vector.tensor_copy, 0, 0, 256)
-        round_pairs(nc.vector.tensor_copy, 0, 256, T)
+        round_pairs(nc.scalar.copy, 0, 256, T)
         round_pairs(nc.scalar.copy, 1, 0, T)
         nc.scalar.copy(token_x[:].rearrange("p (t u) -> p t u", u=2), pairs[:, :, 0:T].rearrange("p u t -> p t u"))
 
-        for u in range(2):
-            for j in range(4):
-                gather(u, j)
+        gather(0, 0, S)
+        for lo, hi in PIECES:
+            gather(1, lo, hi)
         for j in range(4):
             interleave(j)
         quantize_slots(slot_x[0], 0)
@@ -163,7 +158,7 @@ def tile_moe_shr_lin_bias_kernel(tc, xT, w_words, w_scales, b, gate, offs, pos1,
         empty(1, 0)
         for e in (E - 2, E - 1):
             nc.vector.tensor_scalar_add(y[0][:, e * C : (e + 1) * C], place(e, 0), bias[:, 0, e : e + 1])
-        token_codes = keep.tile([P, T], U32, name="token_codes", tag="picked3", align_bytes=64)
+        token_codes = keep.tile([P, T], U32, name="token_codes", tag="picked", align_bytes=64)
         ys_ps = [psum.tile([P, T], F32, name=f"ys_ps{h}", tag=("spare", "bank0_2")[h]) for h in range(HALVES)]
         quantize_tokens(256, 384)
         quantize_tokens(0, 256)

@@ -102,7 +102,7 @@ def tile_moe_shr_lin_bias_kernel(tc, xT, w_words, w_scales, b, gate, offs, pos1,
 
         def quantize_tokens(lo, hi):
             nc.vector.quantize_mx(
-                out=token_codes[:, lo:hi].bitcast(E4M3X4),
+                out=token_codes[lo][:].bitcast(E4M3X4),
                 scales=token_scales[:, lo:hi],
                 in_=token_x[:, 2 * lo : 2 * hi].bitcast(BF16),
             )
@@ -137,7 +137,7 @@ def tile_moe_shr_lin_bias_kernel(tc, xT, w_words, w_scales, b, gate, offs, pos1,
 
         def shared(h):
             for lo, hi in ((256, T), (0, 256)):
-                multiply(ys_ps[h][:, lo:hi], E, h, token_codes[:, lo:hi], token_scales[:, lo:hi])
+                multiply(ys_ps[h][:, lo:hi], E, h, token_codes[lo][:], token_scales[:, lo:hi])
 
         round_pairs(nc.vector.tensor_copy, 0, 0, 256)
         round_pairs(nc.scalar.copy, 0, 256, T)
@@ -158,7 +158,10 @@ def tile_moe_shr_lin_bias_kernel(tc, xT, w_words, w_scales, b, gate, offs, pos1,
         empty(1, 0)
         for e in (E - 2, E - 1):
             nc.vector.tensor_scalar_add(y[0][:, e * C : (e + 1) * C], place(e, 0), bias[:, 0, e : e + 1])
-        token_codes = keep.tile([P, T], U32, name="token_codes", tag="picked", align_bytes=64)
+        token_codes = {
+            0: keep.tile([P, 256], U32, name="token_codes0", tag="picked", align_bytes=64),
+            256: keep.tile([P, T - 256], U32, name="token_codes1", align_bytes=64),
+        }
         ys_ps = [psum.tile([P, T], F32, name=f"ys_ps{h}", tag=("spare", "bank0_2")[h]) for h in range(HALVES)]
         quantize_tokens(256, 384)
         quantize_tokens(0, 256)

@@ -7,6 +7,7 @@ K, T, E, C, N = 512, 384, 6, 128, 256
 S = E * C
 P = 128
 HALVES = N // P
+BLOCKS = T // P
 FLOPS = 2 * K * N * (S + T)
 
 F32 = mybir.dt.float32
@@ -19,10 +20,14 @@ E4M3X4 = mybir.dt.float8_e4m3fn_x4
 E2M1X4 = mybir.dt.float4_e2m1fn_x4
 
 ADD, MULT = mybir.AluOpType.add, mybir.AluOpType.mult
-COPY, IDENTITY = mybir.ActivationFunctionType.Copy, mybir.ActivationFunctionType.Identity
+IDENTITY = mybir.ActivationFunctionType.Identity
 
 WINDOWS = (1024, 512)
-PIECES = ((0, 256), (256, 512), (512, 640), (640, 768))
+PIECES = ((0, 2 * C), (2 * C, 4 * C), (4 * C, 5 * C), (5 * C, S))
+CUT = 2 * P
+PARTS = ((0, CUT), (CUT, T))
+ON_VECTOR = (3, 4)
+BIAS_ROW = 8
 
 
 def tile_moe_shr_lin_bias_kernel(tc, xT, w_words, w_scales, b, gate, offs, pos1, pos2, out):
@@ -31,6 +36,9 @@ def tile_moe_shr_lin_bias_kernel(tc, xT, w_words, w_scales, b, gate, offs, pos1,
         lists = ctx.enter_context(tc.tile_pool(name="lists", bufs=1))
         keep = ctx.enter_context(tc.tile_pool(name="keep", bufs=1))
         psum = ctx.enter_context(tc.psum_pool(name="psum", bufs=1))
+
+        def bank(number, name, columns):
+            return psum.tile([P, columns], F32, name=name, tag=f"bank{number}")
 
         offs_sb = lists.tile([P, S // 16], U16, name="offs_sb")
         pos1_sb = lists.tile([P, T // 16], U16, name="pos1_sb")
@@ -46,7 +54,7 @@ def tile_moe_shr_lin_bias_kernel(tc, xT, w_words, w_scales, b, gate, offs, pos1,
         token_scales = keep.tile([P, T], U8, name="token_scales", align_bytes=64)
         words = keep.tile([P, E + 1, 2 * N], U8, name="words", align_bytes=64)
         scales = keep.tile([P, E + 1, N], U8, name="scales", align_bytes=64)
-        bias = keep.tile([P, HALVES, 8], F32, name="bias")
+        bias = keep.tile([P, HALVES, BIAS_ROW], F32, name="bias")
         gates = keep.tile([P, 2, T], F32, name="gates")
         y = [keep.tile([P, S], F32, name=f"y{h}") for h in range(HALVES)]
         first = [keep.tile([P, T], F32, name=f"first{h}") for h in range(HALVES)]
@@ -56,8 +64,7 @@ def tile_moe_shr_lin_bias_kernel(tc, xT, w_words, w_scales, b, gate, offs, pos1,
         partial = keep.tile([P, T], F32, name="partial")
         identity = keep.tile([P, P], F32, name="identity")
         result = [keep.tile([P, T], F32, name=f"result{h}") for h in range(HALVES)]
-        warm = keep.tile([P, 2], F32, name="warm")
-        y_ps = [[psum.tile([P, 2 * C], F32, name=f"y_ps0_{j}", tag=f"bank0_{j}") for j in range(len(PIECES))]]
+        y0_ps = [bank(e, f"y0_ps{e}", C) for e in range(E)]
 
         x_view = xT.rearrange("(p u i) t -> p u i t", u=2, i=2)
         nc.sync.dma_start(out=x_raw[:, 0], in_=x_view[:, 0])
@@ -65,17 +72,15 @@ def tile_moe_shr_lin_bias_kernel(tc, xT, w_words, w_scales, b, gate, offs, pos1,
         nc.sync.dma_start(out=x_raw[:, 1], in_=x_view[:, 1])
 
         nc.vector.memset(scales[:].rearrange("p e n -> p (e n)").bitcast(I32), 0)
-        nc.vector.memset(warm[:, 0:1], 0.0)
-        nc.scalar.activation(warm[:, 1:2], warm[:, 0:1], IDENTITY)
         for u in range(2):
             nc.gpsimd.memset(pairs[:, u, T : WINDOWS[u]], 0)
         make_identity(nc, identity[:])
 
         w_scales_i = w_scales.bitcast(I32)
-        for q in range(4):
+        for quadrant in range(4):
             nc.sync.dma_start(
-                out=scales[32 * q : 32 * q + 4].bitcast(I32),
-                in_=w_scales_i[:, 0, 4 * q : 4 * q + 4, :].rearrange("e q n -> q e n"),
+                out=scales[32 * quadrant : 32 * quadrant + 4].bitcast(I32),
+                in_=w_scales_i[:, 0, 4 * quadrant : 4 * quadrant + 4, :].rearrange("e q n -> q e n"),
             )
         nc.sync.dma_start(out=words[:].bitcast(I32), in_=w_words.bitcast(I32).rearrange("e a p x -> p (e a) x"))
         nc.sync.dma_start(out=bias[:, :, 0 : E + 1], in_=b.rearrange("(h p) e -> p h e", p=P))
@@ -92,20 +97,11 @@ def tile_moe_shr_lin_bias_kernel(tc, xT, w_words, w_scales, b, gate, offs, pos1,
         def gather(u, lo, hi):
             nc.vector.tensor_copy(picked[:, u, lo:hi], pairs[:, u, 0 : WINDOWS[u]].indirect(offs_sb[:, lo // 16 : hi // 16]))
 
-        def interleave(j):
-            lo, hi = PIECES[j]
-            nc.scalar.copy(slot_x[j][:].rearrange("p (s u) -> p s u", u=2), picked[:, :, lo:hi].rearrange("p u s -> p s u"))
+        def weave(dst, planes):
+            nc.scalar.copy(dst.rearrange("p (c u) -> p c u", u=2), planes.rearrange("p u c -> p c u"))
 
-        def quantize_slots(src, j):
-            lo, hi = PIECES[j]
-            nc.vector.quantize_mx(out=slot_codes[:, lo:hi].bitcast(E4M3X4), scales=slot_scales[:, lo:hi], in_=src[:].bitcast(BF16))
-
-        def quantize_tokens(lo, hi):
-            nc.vector.quantize_mx(
-                out=token_codes[lo][:].bitcast(E4M3X4),
-                scales=token_scales[:, lo:hi],
-                in_=token_x[:, 2 * lo : 2 * hi].bitcast(BF16),
-            )
+        def quantize(codes, code_scales, woven):
+            nc.vector.quantize_mx(out=codes.bitcast(E4M3X4), scales=code_scales, in_=woven.bitcast(BF16))
 
         def multiply(acc, e, h, codes, code_scales):
             nc.tensor.matmul_mx(
@@ -118,61 +114,14 @@ def tile_moe_shr_lin_bias_kernel(tc, xT, w_words, w_scales, b, gate, offs, pos1,
                 stop=True,
             )
 
-        def place(e, h):
-            j = [lo <= e * C < hi for lo, hi in PIECES].index(True)
-            j = min(j, len(y_ps[h]) - 1)
-            at = e * C - PIECES[j][0]
-            return y_ps[h][j][:, at : at + C]
+        def slots(e):
+            return slice(e * C, (e + 1) * C)
 
-        def experts_of(j):
-            return range(PIECES[j][0] // C, PIECES[j][1] // C)
+        def block(j):
+            return slice(j * P, (j + 1) * P)
 
-        def products(j, h):
-            for e in experts_of(j):
-                multiply(place(e, h), e, h, slot_codes[:, e * C : (e + 1) * C], slot_scales[:, e * C : (e + 1) * C])
-
-        def empty(j, h):
-            for e in experts_of(j):
-                nc.scalar.activation(y[h][:, e * C : (e + 1) * C], place(e, h), IDENTITY, bias=bias[:, h, e : e + 1])
-
-        def shared(h):
-            for lo, hi in ((256, T), (0, 256)):
-                multiply(ys_ps[h][:, lo:hi], E, h, token_codes[lo][:], token_scales[:, lo:hi])
-
-        round_pairs(nc.vector.tensor_copy, 0, 0, 256)
-        round_pairs(nc.scalar.copy, 0, 256, T)
-        round_pairs(nc.scalar.copy, 1, 0, T)
-        nc.scalar.copy(token_x[:].rearrange("p (t u) -> p t u", u=2), pairs[:, :, 0:T].rearrange("p u t -> p t u"))
-
-        gather(0, 0, S)
-        for lo, hi in PIECES:
-            gather(1, lo, hi)
-        for j in range(4):
-            interleave(j)
-        quantize_slots(slot_x[0], 0)
-        products(0, 0)
-        empty(0, 0)
-        for j in (1, 2, 3):
-            quantize_slots(slot_x[j], j)
-            products(j, 0)
-        empty(1, 0)
-        for e in (E - 2, E - 1):
-            nc.vector.tensor_scalar_add(y[0][:, e * C : (e + 1) * C], place(e, 0), bias[:, 0, e : e + 1])
-        token_codes = {
-            0: keep.tile([P, 256], U32, name="token_codes0", tag="picked", align_bytes=64),
-            256: keep.tile([P, T - 256], U32, name="token_codes1", align_bytes=64),
-        }
-        ys_ps = [psum.tile([P, T], F32, name=f"ys_ps{h}", tag=("spare", "bank0_2")[h]) for h in range(HALVES)]
-        quantize_tokens(256, 384)
-        quantize_tokens(0, 256)
-        shared(0)
-        nc.scalar.activation(base[:], ys_ps[0][:], IDENTITY, bias=bias[:, 0, E : E + 1])
-        y_ps.append([psum.tile([P, 2 * C], F32, name=f"y_ps1_{j}", tag=("bank0_1", "bank0_0", "bank1_0")[j]) for j in range(3)])
-        for j in range(4):
-            products(j, 1)
-        for j in range(4):
-            empty(j, 1)
-        shared(1)
+        def empty(acc, e, h):
+            nc.scalar.activation(y[h][:, slots(e)], acc, IDENTITY, bias=bias[:, h, e : e + 1])
 
         def fetch(dst, h, g, lo, hi):
             nc.vector.tensor_tensor(
@@ -185,31 +134,72 @@ def tile_moe_shr_lin_bias_kernel(tc, xT, w_words, w_scales, b, gate, offs, pos1,
         def turn(dst, src, start, stop):
             nc.tensor.matmul(dst, lhsT=src, rhs=identity[:], is_transpose=True, start=start, stop=stop)
 
-        def block(j):
-            return slice(j * P, (j + 1) * P)
+        round_pairs(nc.vector.tensor_copy, 0, 0, CUT)
+        round_pairs(nc.scalar.copy, 0, CUT, T)
+        round_pairs(nc.scalar.copy, 1, 0, T)
+        weave(token_x[:], pairs[:, :, 0:T])
 
-        sums = [psum.tile([P, P], F32, name=f"sum{j}", tag=("bank1_1", "bank1_2", "bank0_3")[j]) for j in range(3)]
-        back = [psum.tile([P, hi - lo], F32, name=f"back{lo}", tag=tag) for lo, hi, tag in ((0, 256, "spare"), (256, T, "bank1_0"))]
+        gather(0, 0, S)
+        for lo, hi in PIECES:
+            gather(1, lo, hi)
+        for j, (lo, hi) in enumerate(PIECES):
+            weave(slot_x[j][:], picked[:, :, lo:hi])
+        for j, (lo, hi) in enumerate(PIECES):
+            quantize(slot_codes[:, lo:hi], slot_scales[:, lo:hi], slot_x[j][:])
+            for e in range(lo // C, hi // C):
+                multiply(y0_ps[e][:], e, 0, slot_codes[:, slots(e)], slot_scales[:, slots(e)])
+        for e in range(E):
+            if e not in ON_VECTOR:
+                empty(y0_ps[e][:], e, 0)
+        for e in ON_VECTOR:
+            nc.vector.tensor_scalar_add(y[0][:, slots(e)], y0_ps[e][:], bias[:, 0, e : e + 1])
 
+        token_codes = [
+            keep.tile([P, CUT], U32, name="token_codes_long", tag="picked", align_bytes=64),
+            keep.tile([P, T - CUT], U32, name="token_codes_short", align_bytes=64),
+        ]
+        ys_ps = [bank(6, "ys_ps0", T), bank(4, "ys_ps1", T)]
+        short_first = list(zip(token_codes, PARTS))[::-1]
+
+        def shared(h):
+            for codes, (lo, hi) in short_first:
+                multiply(ys_ps[h][:, lo:hi], E, h, codes[:], token_scales[:, lo:hi])
+
+        for codes, (lo, hi) in short_first:
+            quantize(codes[:], token_scales[:, lo:hi], token_x[:, 2 * lo : 2 * hi])
+        shared(0)
+        nc.scalar.activation(base[:], ys_ps[0][:], IDENTITY, bias=bias[:, 0, E : E + 1])
+
+        y1_ps = [bank(2 - j, f"y1_ps{j}", 2 * C) for j in range(E // 2)]
+        for e in range(E):
+            multiply(y1_ps[e // 2][:, slots(e % 2)], e, 1, slot_codes[:, slots(e)], slot_scales[:, slots(e)])
+        for e in range(E):
+            empty(y1_ps[e // 2][:, slots(e % 2)], e, 1)
+        shared(1)
+
+        sums = [bank(number, f"sum{j}", P) for j, number in enumerate((7, 3, 5))]
+        back = [bank(6, "back_long", CUT), bank(0, "back_short", T - CUT)]
         fetch(first[0], 0, 0, 0, T)
-        for j in range(3):
+        for j in range(BLOCKS):
             turn(sums[j][:], first[0][:, block(j)], True, False)
             turn(sums[j][:], base[:, block(j)], False, False)
-        fetch(second[0], 0, 1, 0, 256)
-        fetch(second[0], 0, 1, 256, T)
-        for j in range(3):
+        for lo, hi in PARTS:
+            fetch(second[0], 0, 1, lo, hi)
+        for j in range(BLOCKS):
             turn(sums[j][:], second[0][:, block(j)], False, True)
-        for j in range(3):
+        for j in range(BLOCKS):
             nc.scalar.copy(turned[:, block(j)], sums[j][:])
-        for j in range(3):
-            turn(back[j // 2][:, block(j % 2)], turned[:, block(j)], True, True)
-        nc.scalar.copy(result[0][:, 0:256], back[0][:])
-        nc.scalar.copy(result[0][:, 256:T], back[1][:])
+        for part, (lo, hi) in zip(back, PARTS):
+            for at in range(lo, hi, P):
+                turn(part[:, at - lo : at - lo + P], turned[:, at : at + P], True, True)
+        for part, (lo, hi) in zip(back, PARTS):
+            nc.scalar.copy(result[0][:, lo:hi], part[:])
         nc.scalar.dma_start(out=out[0:P, :], in_=result[0][:])
+
         fetch(first[1], 1, 0, 0, T)
-        fetch(second[1], 1, 1, 0, 256)
+        fetch(second[1], 1, 1, 0, CUT)
         nc.vector.scalar_tensor_tensor(partial[:], ys_ps[1][:], bias[:, 1, E : E + 1], first[1][:], ADD, ADD)
-        fetch(second[1], 1, 1, 256, T)
-        for lo, hi, queue in ((0, 256, nc.sync), (256, T, nc.sync)):
+        fetch(second[1], 1, 1, CUT, T)
+        for lo, hi in PARTS:
             nc.vector.tensor_tensor(result[1][:, lo:hi], partial[:, lo:hi], second[1][:, lo:hi], ADD)
-            queue.dma_start(out=out[P : 2 * P, lo:hi], in_=result[1][:, lo:hi])
+            nc.sync.dma_start(out=out[P:N, lo:hi], in_=result[1][:, lo:hi])

@@ -137,7 +137,7 @@ def tile_moe_shr_lin_bias_kernel(tc, xT, w_words, w_scales, b, gate, offs, pos1,
         round_pairs(nc.vector.tensor_copy, 0, 0, CUT)
         round_pairs(nc.scalar.copy, 0, CUT, T)
         round_pairs(nc.scalar.copy, 1, 0, T)
-        weave(token_x[:], pairs[:, :, 0:T])
+        nc.gpsimd.tensor_copy(token_x[:].rearrange("p (c u) -> p c u", u=2), pairs[:, :, 0:T].rearrange("p u c -> p c u"))
 
         gather(0, 0, S)
         for lo, hi in PIECES:

@@ -21,12 +21,15 @@ E2M1X4 = mybir.dt.float4_e2m1fn_x4
 
 ADD, MULT = mybir.AluOpType.add, mybir.AluOpType.mult
 IDENTITY = mybir.ActivationFunctionType.Identity
+COPY = mybir.ActivationFunctionType.Copy
 
 WINDOWS = (1024, 512)
 PIECES = ((0, 2 * C), (2 * C, 4 * C), (4 * C, 5 * C), (5 * C, S))
+BY_SCALAR = C
+ROW_WINDOW = 512
 CUT = 2 * P
 PARTS = ((0, CUT), (CUT, T))
-ON_VECTOR = (3, 4)
+ON_VECTOR = ()
 BIAS_ROW = 8
 
 
@@ -46,8 +49,10 @@ def tile_moe_shr_lin_bias_kernel(tc, xT, w_words, w_scales, b, gate, offs, pos1,
 
         x_raw = keep.tile([P, 2, 2, T], F32, name="x_raw")
         pairs = keep.tile([P, 2, WINDOWS[0]], U32, name="pairs")
-        picked = keep.tile([P, 2, S], U32, name="picked", tag="picked", align_bytes=64)
+        picked = keep.tile([P, 2, S - BY_SCALAR], U32, name="picked", tag="picked", align_bytes=64)
+        picked_late = keep.tile([P, 2 * BY_SCALAR], U32, name="picked_late")
         slot_x = [keep.tile([P, 2 * (hi - lo)], U32, name=f"slot_x{j}", align_bytes=64) for j, (lo, hi) in enumerate(PIECES)]
+        rows = keep.tile([P, 2, ROW_WINDOW], BF16, name="rows")
         token_x = keep.tile([P, 2 * T], U32, name="token_x", align_bytes=64)
         slot_codes = keep.tile([P, S], U32, name="slot_codes", align_bytes=64)
         slot_scales = keep.tile([P, S], U8, name="slot_scales", align_bytes=64)
@@ -74,6 +79,7 @@ def tile_moe_shr_lin_bias_kernel(tc, xT, w_words, w_scales, b, gate, offs, pos1,
         nc.vector.memset(scales[:].rearrange("p e n -> p (e n)").bitcast(I32), 0)
         for u in range(2):
             nc.gpsimd.memset(pairs[:, u, T : WINDOWS[u]], 0)
+        nc.gpsimd.memset(rows[:, :, T:ROW_WINDOW], 0)
         make_identity(nc, identity[:])
 
         w_scales_i = w_scales.bitcast(I32)
@@ -95,7 +101,8 @@ def tile_moe_shr_lin_bias_kernel(tc, xT, w_words, w_scales, b, gate, offs, pos1,
             )
 
         def gather(u, lo, hi):
-            nc.vector.tensor_copy(picked[:, u, lo:hi], pairs[:, u, 0 : WINDOWS[u]].indirect(offs_sb[:, lo // 16 : hi // 16]))
+            dst = picked[:, u, lo:hi] if hi <= S - BY_SCALAR else picked_late[:, BY_SCALAR:]
+            nc.vector.tensor_copy(dst, pairs[:, u, 0 : WINDOWS[u]].indirect(offs_sb[:, lo // 16 : hi // 16]))
 
         def weave(dst, planes):
             nc.scalar.copy(dst.rearrange("p (c u) -> p c u", u=2), planes.rearrange("p u c -> p c u"))
@@ -136,14 +143,18 @@ def tile_moe_shr_lin_bias_kernel(tc, xT, w_words, w_scales, b, gate, offs, pos1,
 
         round_pairs(nc.vector.tensor_copy, 0, 0, CUT)
         round_pairs(nc.scalar.copy, 0, CUT, T)
+        nc.scalar.copy(rows[:, :, 0:T], x_raw[:, 0])
         round_pairs(nc.scalar.copy, 1, 0, T)
+        late = picked_late[:, 0:BY_SCALAR].bitcast(BF16).rearrange("p (c i) -> p i c", i=2)
+        for i in range(2):
+            nc.scalar.activation(late[:, i, :], rows[:, i, :].indirect(offs_sb[:, (S - BY_SCALAR) // 16 : S // 16]), COPY)
         nc.gpsimd.tensor_copy(token_x[:].rearrange("p (c u) -> p c u", u=2), pairs[:, :, 0:T].rearrange("p u c -> p c u"))
 
-        gather(0, 0, S)
+        gather(0, 0, S - BY_SCALAR)
         for lo, hi in PIECES:
             gather(1, lo, hi)
         for j, (lo, hi) in enumerate(PIECES):
-            weave(slot_x[j][:], picked[:, :, lo:hi])
+            weave(slot_x[j][:], picked[:, :, lo:hi] if hi < S else picked_late[:].rearrange("p (u c) -> p u c", u=2))
         for j, (lo, hi) in enumerate(PIECES):
             quantize(slot_codes[:, lo:hi], slot_scales[:, lo:hi], slot_x[j][:])
             for e in range(lo // C, hi // C):

@@ -25,7 +25,7 @@ COPY = mybir.ActivationFunctionType.Copy
 
 WINDOWS = (1024, 512)
 PIECES = ((0, 2 * C), (2 * C, 4 * C), (4 * C, 5 * C), (5 * C, S))
-BY_SCALAR = C
+BY_SCALAR = 2 * C
 ROW_WINDOW = 512
 CUT = 2 * P
 PARTS = ((0, CUT), (CUT, T))
@@ -38,6 +38,7 @@ def tile_moe_shr_lin_bias_kernel(tc, xT, w_words, w_scales, b, gate, offs, pos1,
     with ExitStack() as ctx:
         lists = ctx.enter_context(tc.tile_pool(name="lists", bufs=1))
         keep = ctx.enter_context(tc.tile_pool(name="keep", bufs=1))
+        shared_bytes = ctx.enter_context(tc.tile_pool(name="shared_bytes", bufs=1))
         psum = ctx.enter_context(tc.psum_pool(name="psum", bufs=1))
 
         def bank(number, name, columns):
@@ -49,8 +50,8 @@ def tile_moe_shr_lin_bias_kernel(tc, xT, w_words, w_scales, b, gate, offs, pos1,
 
         x_raw = keep.tile([P, 2, 2, T], F32, name="x_raw")
         pairs = keep.tile([P, 2, WINDOWS[0]], U32, name="pairs")
-        picked = keep.tile([P, 2, S - BY_SCALAR], U32, name="picked", tag="picked", align_bytes=64)
-        picked_late = keep.tile([P, 2 * BY_SCALAR], U32, name="picked_late")
+        picked = keep.tile([P, 2, S - BY_SCALAR], U32, name="picked")
+        picked_late = shared_bytes.tile([P, 2, BY_SCALAR], U32, name="picked_late", align_bytes=64, offset=0)
         slot_x = [keep.tile([P, 2 * (hi - lo)], U32, name=f"slot_x{j}", align_bytes=64) for j, (lo, hi) in enumerate(PIECES)]
         rows = keep.tile([P, 2, ROW_WINDOW], BF16, name="rows")
         token_x = keep.tile([P, 2 * T], U32, name="token_x", align_bytes=64)
@@ -61,7 +62,10 @@ def tile_moe_shr_lin_bias_kernel(tc, xT, w_words, w_scales, b, gate, offs, pos1,
         scales = keep.tile([P, E + 1, N], U8, name="scales", align_bytes=64)
         bias = keep.tile([P, HALVES, BIAS_ROW], F32, name="bias")
         gates = keep.tile([P, 2, T], F32, name="gates")
-        y = [keep.tile([P, S], F32, name=f"y{h}") for h in range(HALVES)]
+        y = [
+            shared_bytes.tile([P, S], F32, name="y0", align_bytes=64, offset=4 * CUT),
+            keep.tile([P, S], F32, name="y1"),
+        ]
         first = [keep.tile([P, T], F32, name=f"first{h}") for h in range(HALVES)]
         second = [keep.tile([P, T], F32, name=f"second{h}") for h in range(HALVES)]
         base = keep.tile([P, T], F32, name="base")
@@ -101,7 +105,7 @@ def tile_moe_shr_lin_bias_kernel(tc, xT, w_words, w_scales, b, gate, offs, pos1,
             )
 
         def gather(u, lo, hi):
-            dst = picked[:, u, lo:hi] if hi <= S - BY_SCALAR else picked_late[:, BY_SCALAR:]
+            dst = picked[:, u, lo:hi] if hi <= S - BY_SCALAR else picked_late[:, u, lo - S + BY_SCALAR : hi - S + BY_SCALAR]
             nc.vector.tensor_copy(dst, pairs[:, u, 0 : WINDOWS[u]].indirect(offs_sb[:, lo // 16 : hi // 16]))
 
         def weave(dst, planes):
@@ -144,8 +148,9 @@ def tile_moe_shr_lin_bias_kernel(tc, xT, w_words, w_scales, b, gate, offs, pos1,
         round_pairs(nc.vector.tensor_copy, 0, 0, CUT)
         round_pairs(nc.scalar.copy, 0, CUT, T)
         nc.scalar.copy(rows[:, :, 0:T], x_raw[:, 0])
-        round_pairs(nc.scalar.copy, 1, 0, T)
-        late = picked_late[:, 0:BY_SCALAR].bitcast(BF16).rearrange("p (c i) -> p i c", i=2)
+        round_pairs(nc.gpsimd.tensor_copy, 1, 0, CUT)
+        round_pairs(nc.scalar.copy, 1, CUT, T)
+        late = picked_late[:, 0, :].bitcast(BF16).rearrange("p (c i) -> p i c", i=2)
         for i in range(2):
             nc.scalar.activation(late[:, i, :], rows[:, i, :].indirect(offs_sb[:, (S - BY_SCALAR) // 16 : S // 16]), COPY)
         nc.gpsimd.tensor_copy(token_x[:].rearrange("p (c u) -> p c u", u=2), pairs[:, :, 0:T].rearrange("p u c -> p c u"))
@@ -154,7 +159,7 @@ def tile_moe_shr_lin_bias_kernel(tc, xT, w_words, w_scales, b, gate, offs, pos1,
         for lo, hi in PIECES:
             gather(1, lo, hi)
         for j, (lo, hi) in enumerate(PIECES):
-            weave(slot_x[j][:], picked[:, :, lo:hi] if hi < S else picked_late[:].rearrange("p (u c) -> p u c", u=2))
+            weave(slot_x[j][:], picked[:, :, lo:hi] if hi <= S - BY_SCALAR else picked_late[:, :, lo - S + BY_SCALAR : hi - S + BY_SCALAR])
         for j, (lo, hi) in enumerate(PIECES):
             quantize(slot_codes[:, lo:hi], slot_scales[:, lo:hi], slot_x[j][:])
             for e in range(lo // C, hi // C):
@@ -166,10 +171,10 @@ def tile_moe_shr_lin_bias_kernel(tc, xT, w_words, w_scales, b, gate, offs, pos1,
             nc.vector.tensor_scalar_add(y[0][:, slots(e)], y0_ps[e][:], bias[:, 0, e : e + 1])
 
         token_codes = [
-            keep.tile([P, CUT], U32, name="token_codes_long", tag="picked", align_bytes=64),
+            shared_bytes.tile([P, CUT], U32, name="token_codes_long", align_bytes=64, offset=0),
             keep.tile([P, T - CUT], U32, name="token_codes_short", align_bytes=64),
         ]
-        ys_ps = [bank(6, "ys_ps0", T), bank(4, "ys_ps1", T)]
+        ys_ps = [bank(6, "ys_ps0", T), bank(0, "ys_ps1", T)]
         short_first = list(zip(token_codes, PARTS))[::-1]
 
         def shared(h):
@@ -181,15 +186,15 @@ def tile_moe_shr_lin_bias_kernel(tc, xT, w_words, w_scales, b, gate, offs, pos1,
         shared(0)
         nc.scalar.activation(base[:], ys_ps[0][:], IDENTITY, bias=bias[:, 0, E : E + 1])
 
-        y1_ps = [bank(2 - j, f"y1_ps{j}", 2 * C) for j in range(E // 2)]
+        y1_ps = [bank(3 + j, f"y1_ps{j}", 2 * C) for j in range(E // 2)]
         for e in range(E):
             multiply(y1_ps[e // 2][:, slots(e % 2)], e, 1, slot_codes[:, slots(e)], slot_scales[:, slots(e)])
         for e in range(E):
             empty(y1_ps[e // 2][:, slots(e % 2)], e, 1)
         shared(1)
 
-        sums = [bank(number, f"sum{j}", P) for j, number in enumerate((7, 3, 5))]
-        back = [bank(6, "back_long", CUT), bank(0, "back_short", T - CUT)]
+        sums = [bank(number, f"sum{j}", P) for j, number in enumerate((7, 1, 2))]
+        back = [bank(6, "back_long", CUT), bank(3, "back_short", T - CUT)]
         fetch(first[0], 0, 0, 0, T)
         for j in range(BLOCKS):
             turn(sums[j][:], first[0][:, block(j)], True, False)

@@ -25,7 +25,7 @@ COPY = mybir.ActivationFunctionType.Copy
 
 WINDOWS = (1024, 512)
 PIECES = ((0, 2 * C), (2 * C, 4 * C), (4 * C, 5 * C), (5 * C, S))
-BY_SCALAR = 2 * C
+BY_SCALAR = 320
 ROW_WINDOW = 512
 CUT = 2 * P
 PARTS = ((0, CUT), (CUT, T))
@@ -50,12 +50,14 @@ def tile_moe_shr_lin_bias_kernel(tc, xT, w_words, w_scales, b, gate, offs, pos1,
 
         x_raw = keep.tile([P, 2, 2, T], F32, name="x_raw")
         pairs = keep.tile([P, 2, WINDOWS[0]], U32, name="pairs")
-        picked = keep.tile([P, 2, S - BY_SCALAR], U32, name="picked")
-        picked_late = shared_bytes.tile([P, 2, BY_SCALAR], U32, name="picked_late", align_bytes=64, offset=0)
-        slot_x = [keep.tile([P, 2 * (hi - lo)], U32, name=f"slot_x{j}", align_bytes=64) for j, (lo, hi) in enumerate(PIECES)]
+        picked = shared_bytes.tile([P, 2, S], U32, name="picked", align_bytes=64, offset=0)
+        slot_x = [shared_bytes.tile([P, 4 * C], U32, name="slot_x0", align_bytes=64, offset=8192)]
+        slot_x += [keep.tile([P, 4 * C], U32, name="slot_x1", align_bytes=64)]
+        slot_x += [shared_bytes.tile([P, 2 * C], U32, name=f"slot_x{j}", align_bytes=64, offset=8192 + 1024 * j) for j in (2, 3)]
         rows = keep.tile([P, 2, ROW_WINDOW], BF16, name="rows")
         token_x = keep.tile([P, 2 * T], U32, name="token_x", align_bytes=64)
-        slot_codes = keep.tile([P, S], U32, name="slot_codes", align_bytes=64)
+        codes_first = keep.tile([P, 2 * C], U32, name="codes_first", align_bytes=64)
+        codes_rest = shared_bytes.tile([P, S - 2 * C], U32, name="codes_rest", align_bytes=64, offset=8192)
         slot_scales = keep.tile([P, S], U8, name="slot_scales", align_bytes=64)
         token_scales = keep.tile([P, T], U8, name="token_scales", align_bytes=64)
         words = keep.tile([P, E + 1, 2 * N], U8, name="words", align_bytes=64)
@@ -63,7 +65,7 @@ def tile_moe_shr_lin_bias_kernel(tc, xT, w_words, w_scales, b, gate, offs, pos1,
         bias = keep.tile([P, HALVES, BIAS_ROW], F32, name="bias")
         gates = keep.tile([P, 2, T], F32, name="gates")
         y = [
-            shared_bytes.tile([P, S], F32, name="y0", align_bytes=64, offset=4 * CUT),
+            shared_bytes.tile([P, S], F32, name="y0", align_bytes=64, offset=0),
             keep.tile([P, S], F32, name="y1"),
         ]
         first = [keep.tile([P, T], F32, name=f"first{h}") for h in range(HALVES)]
@@ -105,11 +107,10 @@ def tile_moe_shr_lin_bias_kernel(tc, xT, w_words, w_scales, b, gate, offs, pos1,
             )
 
         def gather(u, lo, hi):
-            dst = picked[:, u, lo:hi] if hi <= S - BY_SCALAR else picked_late[:, u, lo - S + BY_SCALAR : hi - S + BY_SCALAR]
-            nc.vector.tensor_copy(dst, pairs[:, u, 0 : WINDOWS[u]].indirect(offs_sb[:, lo // 16 : hi // 16]))
+            nc.vector.tensor_copy(picked[:, u, lo:hi], pairs[:, u, 0 : WINDOWS[u]].indirect(offs_sb[:, lo // 16 : hi // 16]))
 
-        def weave(dst, planes):
-            nc.scalar.copy(dst.rearrange("p (c u) -> p c u", u=2), planes.rearrange("p u c -> p c u"))
+        def weave(engine_copy, dst, planes):
+            engine_copy(dst.rearrange("p (c u) -> p c u", u=2), planes.rearrange("p u c -> p c u"))
 
         def quantize(codes, code_scales, woven):
             nc.vector.quantize_mx(out=codes.bitcast(E4M3X4), scales=code_scales, in_=woven.bitcast(BF16))
@@ -127,6 +128,9 @@ def tile_moe_shr_lin_bias_kernel(tc, xT, w_words, w_scales, b, gate, offs, pos1,
 
         def slots(e):
             return slice(e * C, (e + 1) * C)
+
+        def slot_codes(lo, hi):
+            return codes_first[:, lo:hi] if hi <= 2 * C else codes_rest[:, lo - 2 * C : hi - 2 * C]
 
         def block(j):
             return slice(j * P, (j + 1) * P)
@@ -150,7 +154,7 @@ def tile_moe_shr_lin_bias_kernel(tc, xT, w_words, w_scales, b, gate, offs, pos1,
         nc.scalar.copy(rows[:, :, 0:T], x_raw[:, 0])
         round_pairs(nc.gpsimd.tensor_copy, 1, 0, CUT)
         round_pairs(nc.scalar.copy, 1, CUT, T)
-        late = picked_late[:, 0, :].bitcast(BF16).rearrange("p (c i) -> p i c", i=2)
+        late = picked[:, 0, S - BY_SCALAR : S].bitcast(BF16).rearrange("p (c i) -> p i c", i=2)
         for i in range(2):
             nc.scalar.activation(late[:, i, :], rows[:, i, :].indirect(offs_sb[:, (S - BY_SCALAR) // 16 : S // 16]), COPY)
         nc.gpsimd.tensor_copy(token_x[:].rearrange("p (c u) -> p c u", u=2), pairs[:, :, 0:T].rearrange("p u c -> p c u"))
@@ -159,11 +163,11 @@ def tile_moe_shr_lin_bias_kernel(tc, xT, w_words, w_scales, b, gate, offs, pos1,
         for lo, hi in PIECES:
             gather(1, lo, hi)
         for j, (lo, hi) in enumerate(PIECES):
-            weave(slot_x[j][:], picked[:, :, lo:hi] if hi <= S - BY_SCALAR else picked_late[:, :, lo - S + BY_SCALAR : hi - S + BY_SCALAR])
+            weave(nc.scalar.copy if j else nc.gpsimd.tensor_copy, slot_x[j][:], picked[:, :, lo:hi])
         for j, (lo, hi) in enumerate(PIECES):
-            quantize(slot_codes[:, lo:hi], slot_scales[:, lo:hi], slot_x[j][:])
+            quantize(slot_codes(lo, hi), slot_scales[:, lo:hi], slot_x[j][:])
             for e in range(lo // C, hi // C):
-                multiply(y0_ps[e][:], e, 0, slot_codes[:, slots(e)], slot_scales[:, slots(e)])
+                multiply(y0_ps[e][:], e, 0, slot_codes(e * C, (e + 1) * C), slot_scales[:, slots(e)])
         for e in range(E):
             if e not in ON_VECTOR:
                 empty(y0_ps[e][:], e, 0)
@@ -171,8 +175,8 @@ def tile_moe_shr_lin_bias_kernel(tc, xT, w_words, w_scales, b, gate, offs, pos1,
             nc.vector.tensor_scalar_add(y[0][:, slots(e)], y0_ps[e][:], bias[:, 0, e : e + 1])
 
         token_codes = [
-            shared_bytes.tile([P, CUT], U32, name="token_codes_long", align_bytes=64, offset=0),
-            keep.tile([P, T - CUT], U32, name="token_codes_short", align_bytes=64),
+            shared_bytes.tile([P, CUT], U32, name="token_codes_long", align_bytes=64, offset=8192 + 1024 * 3),
+            shared_bytes.tile([P, T - CUT], U32, name="token_codes_short", align_bytes=64, offset=8192 + 1024 * 2),
         ]
         ys_ps = [bank(6, "ys_ps0", T), bank(0, "ys_ps1", T)]
         short_first = list(zip(token_codes, PARTS))[::-1]
@@ -188,7 +192,7 @@ def tile_moe_shr_lin_bias_kernel(tc, xT, w_words, w_scales, b, gate, offs, pos1,
 
         y1_ps = [bank(3 + j, f"y1_ps{j}", 2 * C) for j in range(E // 2)]
         for e in range(E):
-            multiply(y1_ps[e // 2][:, slots(e % 2)], e, 1, slot_codes[:, slots(e)], slot_scales[:, slots(e)])
+            multiply(y1_ps[e // 2][:, slots(e % 2)], e, 1, slot_codes(e * C, (e + 1) * C), slot_scales[:, slots(e)])
         for e in range(E):
             empty(y1_ps[e // 2][:, slots(e % 2)], e, 1)
         shared(1)

@@ -24,12 +24,11 @@ IDENTITY = mybir.ActivationFunctionType.Identity
 COPY = mybir.ActivationFunctionType.Copy
 
 WINDOWS = (1024, 512)
-PIECES = ((0, 2 * C), (2 * C, 4 * C), (4 * C, 5 * C), (5 * C, S))
-BY_SCALAR = 320
 ROW_WINDOW = 512
+BY_SCALAR = 2 * C
+PIECES = ((0, 2 * C), (2 * C, 4 * C), (4 * C, 5 * C), (5 * C, S))
 CUT = 2 * P
 PARTS = ((0, CUT), (CUT, T))
-ON_VECTOR = ()
 BIAS_ROW = 8
 
 
@@ -38,11 +37,16 @@ def tile_moe_shr_lin_bias_kernel(tc, xT, w_words, w_scales, b, gate, offs, pos1,
     with ExitStack() as ctx:
         lists = ctx.enter_context(tc.tile_pool(name="lists", bufs=1))
         keep = ctx.enter_context(tc.tile_pool(name="keep", bufs=1))
-        shared_bytes = ctx.enter_context(tc.tile_pool(name="shared_bytes", bufs=1))
+        reused = ctx.enter_context(tc.tile_pool(name="reused", bufs=1))
         psum = ctx.enter_context(tc.psum_pool(name="psum", bufs=1))
 
         def bank(number, name, columns):
             return psum.tile([P, columns], F32, name=name, tag=f"bank{number}")
+
+        def reuse(name, shape, dtype, offset):
+            return reused.tile(shape, dtype, name=name, align_bytes=64, offset=offset)
+
+        woven_at = {j: 8 * (S + PIECES[j][0]) for j in (0, 2, 3)}
 
         offs_sb = lists.tile([P, S // 16], U16, name="offs_sb")
         pos1_sb = lists.tile([P, T // 16], U16, name="pos1_sb")
@@ -50,24 +54,24 @@ def tile_moe_shr_lin_bias_kernel(tc, xT, w_words, w_scales, b, gate, offs, pos1,
 
         x_raw = keep.tile([P, 2, 2, T], F32, name="x_raw")
         pairs = keep.tile([P, 2, WINDOWS[0]], U32, name="pairs")
-        picked = shared_bytes.tile([P, 2, S], U32, name="picked", align_bytes=64, offset=0)
-        slot_x = [shared_bytes.tile([P, 4 * C], U32, name="slot_x0", align_bytes=64, offset=8192)]
-        slot_x += [keep.tile([P, 4 * C], U32, name="slot_x1", align_bytes=64)]
-        slot_x += [shared_bytes.tile([P, 2 * C], U32, name=f"slot_x{j}", align_bytes=64, offset=8192 + 1024 * j) for j in (2, 3)]
+        picked = reuse("picked", [P, 2, S], U32, 0)
+        slot_x = [
+            reuse(f"slot_x{j}", [P, 2 * (hi - lo)], U32, woven_at[j])
+            if j in woven_at
+            else keep.tile([P, 2 * (hi - lo)], U32, name=f"slot_x{j}", align_bytes=64)
+            for j, (lo, hi) in enumerate(PIECES)
+        ]
         rows = keep.tile([P, 2, ROW_WINDOW], BF16, name="rows")
         token_x = keep.tile([P, 2 * T], U32, name="token_x", align_bytes=64)
         codes_first = keep.tile([P, 2 * C], U32, name="codes_first", align_bytes=64)
-        codes_rest = shared_bytes.tile([P, S - 2 * C], U32, name="codes_rest", align_bytes=64, offset=8192)
+        codes_rest = reuse("codes_rest", [P, S - 2 * C], U32, woven_at[0])
         slot_scales = keep.tile([P, S], U8, name="slot_scales", align_bytes=64)
         token_scales = keep.tile([P, T], U8, name="token_scales", align_bytes=64)
         words = keep.tile([P, E + 1, 2 * N], U8, name="words", align_bytes=64)
         scales = keep.tile([P, E + 1, N], U8, name="scales", align_bytes=64)
         bias = keep.tile([P, HALVES, BIAS_ROW], F32, name="bias")
         gates = keep.tile([P, 2, T], F32, name="gates")
-        y = [
-            shared_bytes.tile([P, S], F32, name="y0", align_bytes=64, offset=0),
-            keep.tile([P, S], F32, name="y1"),
-        ]
+        y = [reuse("y0", [P, S], F32, 0), keep.tile([P, S], F32, name="y1")]
         first = [keep.tile([P, T], F32, name=f"first{h}") for h in range(HALVES)]
         second = [keep.tile([P, T], F32, name=f"second{h}") for h in range(HALVES)]
         base = keep.tile([P, T], F32, name="base")
@@ -157,7 +161,7 @@ def tile_moe_shr_lin_bias_kernel(tc, xT, w_words, w_scales, b, gate, offs, pos1,
         late = picked[:, 0, S - BY_SCALAR : S].bitcast(BF16).rearrange("p (c i) -> p i c", i=2)
         for i in range(2):
             nc.scalar.activation(late[:, i, :], rows[:, i, :].indirect(offs_sb[:, (S - BY_SCALAR) // 16 : S // 16]), COPY)
-        nc.gpsimd.tensor_copy(token_x[:].rearrange("p (c u) -> p c u", u=2), pairs[:, :, 0:T].rearrange("p u c -> p c u"))
+        weave(nc.gpsimd.tensor_copy, token_x[:], pairs[:, :, 0:T])
 
         gather(0, 0, S - BY_SCALAR)
         for lo, hi in PIECES:
@@ -169,14 +173,11 @@ def tile_moe_shr_lin_bias_kernel(tc, xT, w_words, w_scales, b, gate, offs, pos1,
             for e in range(lo // C, hi // C):
                 multiply(y0_ps[e][:], e, 0, slot_codes(e * C, (e + 1) * C), slot_scales[:, slots(e)])
         for e in range(E):
-            if e not in ON_VECTOR:
-                empty(y0_ps[e][:], e, 0)
-        for e in ON_VECTOR:
-            nc.vector.tensor_scalar_add(y[0][:, slots(e)], y0_ps[e][:], bias[:, 0, e : e + 1])
+            empty(y0_ps[e][:], e, 0)
 
         token_codes = [
-            shared_bytes.tile([P, CUT], U32, name="token_codes_long", align_bytes=64, offset=8192 + 1024 * 3),
-            shared_bytes.tile([P, T - CUT], U32, name="token_codes_short", align_bytes=64, offset=8192 + 1024 * 2),
+            reuse("token_codes_long", [P, CUT], U32, woven_at[3]),
+            reuse("token_codes_short", [P, T - CUT], U32, woven_at[2]),
         ]
         ys_ps = [bank(6, "ys_ps0", T), bank(0, "ys_ps1", T)]
         short_first = list(zip(token_codes, PARTS))[::-1]

@@ -156,8 +156,8 @@ def tile_moe_shr_lin_bias_kernel(tc, xT, w_words, w_scales, b, gate, offs, pos1,
         round_pairs(nc.vector.tensor_copy, 0, 0, CUT)
         round_pairs(nc.scalar.copy, 0, CUT, T)
         nc.scalar.copy(rows[:, :, 0:T], x_raw[:, 0])
-        round_pairs(nc.gpsimd.tensor_copy, 1, 0, CUT)
-        round_pairs(nc.scalar.copy, 1, CUT, T)
+        round_pairs(nc.gpsimd.tensor_copy, 1, 0, T // 2)
+        round_pairs(nc.scalar.copy, 1, T // 2, T)
         late = picked[:, 0, S - BY_SCALAR : S].bitcast(BF16).rearrange("p (c i) -> p i c", i=2)
         for i in range(2):
             nc.scalar.activation(late[:, i, :], rows[:, i, :].indirect(offs_sb[:, (S - BY_SCALAR) // 16 : S // 16]), COPY)

@@ -74,7 +74,7 @@ def tile_moe_shr_lin_bias_kernel(tc, xT, w_words, w_scales, b, gate, offs, pos1,
         y = [reuse("y0", [P, S], F32, 0), keep.tile([P, S], F32, name="y1")]
         first = [keep.tile([P, T], F32, name=f"first{h}") for h in range(HALVES)]
         second = [keep.tile([P, T], F32, name=f"second{h}") for h in range(HALVES)]
-        base = keep.tile([P, T], F32, name="base")
+        base = reuse("base", [P, T], F32, woven_at[0])
         turned = keep.tile([P, T], F32, name="turned")
         partial = keep.tile([P, T], F32, name="partial")
         identity = keep.tile([P, P], F32, name="identity")
@@ -182,40 +182,49 @@ def tile_moe_shr_lin_bias_kernel(tc, xT, w_words, w_scales, b, gate, offs, pos1,
         ys_ps = [bank(6, "ys_ps0", T), bank(0, "ys_ps1", T)]
         short_first = list(zip(token_codes, PARTS))[::-1]
 
-        def shared(h):
-            for codes, (lo, hi) in short_first:
-                multiply(ys_ps[h][:, lo:hi], E, h, codes[:], token_scales[:, lo:hi])
 
         for codes, (lo, hi) in short_first:
             quantize(codes[:], token_scales[:, lo:hi], token_x[:, 2 * lo : 2 * hi])
-        shared(0)
-        nc.scalar.activation(base[:], ys_ps[0][:], IDENTITY, bias=bias[:, 0, E : E + 1])
+        for codes, (lo, hi) in short_first:
+            for at in range(lo, hi, P):
+                nc.tensor.matmul_mx(
+                    out=ys_ps[0][:, at : at + P],
+                    lhsT=codes[:, at - lo : at - lo + P].bitcast(E4M3X4),
+                    lhsT_scale=token_scales[:, at : at + P],
+                    rhs=words[:, E, 0 : 2 * P].bitcast(E2M1X4),
+                    rhs_scale=scales[:, E, 0:P],
+                    start=True,
+                    stop=True,
+                )
 
         y1_ps = [bank(3 + j, f"y1_ps{j}", 2 * C) for j in range(E // 2)]
         for e in range(E):
             multiply(y1_ps[e // 2][:, slots(e % 2)], e, 1, slot_codes(e * C, (e + 1) * C), slot_scales[:, slots(e)])
         for e in range(E):
             empty(y1_ps[e // 2][:, slots(e % 2)], e, 1)
-        shared(1)
+        for codes, (lo, hi) in short_first:
+            multiply(ys_ps[1][:, lo:hi], E, 1, codes[:], token_scales[:, lo:hi])
+        nc.scalar.copy(base[:], ys_ps[0][:])
 
         sums = [bank(number, f"sum{j}", P) for j, number in enumerate((7, 1, 2))]
-        back = [bank(6, "back_long", CUT), bank(3, "back_short", T - CUT)]
+        back = [bank(number, f"back{j}", P) for j, number in enumerate((3, 4, 6))]
         fetch(first[0], 0, 0, 0, T)
         for j in range(BLOCKS):
             turn(sums[j][:], first[0][:, block(j)], True, False)
-            turn(sums[j][:], base[:, block(j)], False, False)
         for lo, hi in PARTS:
             fetch(second[0], 0, 1, lo, hi)
         for j in range(BLOCKS):
             turn(sums[j][:], second[0][:, block(j)], False, True)
         for j in range(BLOCKS):
+            turn(back[j][:], base[:, block(j)], True, False)
+        for j in range(BLOCKS):
             nc.scalar.copy(turned[:, block(j)], sums[j][:])
-        for part, (lo, hi) in zip(back, PARTS):
-            for at in range(lo, hi, P):
-                turn(part[:, at - lo : at - lo + P], turned[:, at : at + P], True, True)
-        for part, (lo, hi) in zip(back, PARTS):
-            nc.scalar.copy(result[0][:, lo:hi], part[:])
-        nc.scalar.dma_start(out=out[0:P, :], in_=result[0][:])
+        for j in range(BLOCKS):
+            turn(back[j][:], turned[:, block(j)], False, True)
+        for lo, hi in PARTS:
+            for j in range(lo // P, hi // P):
+                nc.scalar.activation(result[0][:, block(j)], back[j][:], IDENTITY, bias=bias[:, 0, E : E + 1])
+            nc.scalar.dma_start(out=out[0:P, lo:hi], in_=result[0][:, lo:hi])
 
         fetch(first[1], 1, 0, 0, T)
         fetch(second[1], 1, 1, 0, CUT)

@@ -23,12 +23,16 @@ ADD, MULT = mybir.AluOpType.add, mybir.AluOpType.mult
 IDENTITY = mybir.ActivationFunctionType.Identity
 COPY = mybir.ActivationFunctionType.Copy
 
-WINDOWS = (1024, 512)
+WINDOWS = (512, 512)
 ROW_WINDOW = 512
-BY_SCALAR = 2 * C
 PIECES = ((0, 2 * C), (2 * C, 4 * C), (4 * C, 5 * C), (5 * C, S))
+BY_SCALAR = 320
+EARLY = 2 * C
+BY_GPSIMD = ((0, EARLY),)
+SCALAR_WEAVES = PIECES[1:]
 CUT = 2 * P
 PARTS = ((0, CUT), (CUT, T))
+LAST_AT = 8 * S + 8 * C
 BIAS_ROW = 8
 
 
@@ -46,35 +50,35 @@ def tile_moe_shr_lin_bias_kernel(tc, xT, w_words, w_scales, b, gate, offs, pos1,
         def reuse(name, shape, dtype, offset):
             return reused.tile(shape, dtype, name=name, align_bytes=64, offset=offset)
 
-        woven_at = {j: 8 * (S + PIECES[j][0]) for j in (0, 2, 3)}
-
         offs_sb = lists.tile([P, S // 16], U16, name="offs_sb")
         pos1_sb = lists.tile([P, T // 16], U16, name="pos1_sb")
         pos2_sb = lists.tile([P, T // 16], U16, name="pos2_sb")
 
         x_raw = keep.tile([P, 2, 2, T], F32, name="x_raw")
         pairs = keep.tile([P, 2, WINDOWS[0]], U32, name="pairs")
-        picked = reuse("picked", [P, 2, S], U32, 0)
-        slot_x = [
-            reuse(f"slot_x{j}", [P, 2 * (hi - lo)], U32, woven_at[j])
-            if j in woven_at
-            else keep.tile([P, 2 * (hi - lo)], U32, name=f"slot_x{j}", align_bytes=64)
-            for j, (lo, hi) in enumerate(PIECES)
-        ]
-        rows = keep.tile([P, 2, ROW_WINDOW], BF16, name="rows")
-        token_x = keep.tile([P, 2 * T], U32, name="token_x", align_bytes=64)
+        early = reuse("early", [P, 2, EARLY], U32, 0)
+        late = reuse("late", [P, 2, S - EARLY], U32, 8 * EARLY)
+        slot_x = keep.tile([P, 2 * (S - 2 * C)], U32, name="slot_x", align_bytes=64)
+        third_x = reuse("third_x", [P, 2 * C], U32, LAST_AT - 8 * C)
+        last_x = reuse("last_x", [P, 2 * C], U32, LAST_AT)
+        rows = [keep.tile([P, ROW_WINDOW], BF16, name=f"row{i}") for i in range(2)]
         codes_first = keep.tile([P, 2 * C], U32, name="codes_first", align_bytes=64)
-        codes_rest = reuse("codes_rest", [P, S - 2 * C], U32, woven_at[0])
+        codes_rest = reuse("codes_rest", [P, S - 2 * C], U32, 0)
+        token_x = keep.tile([P, 2 * T], U32, name="token_x", align_bytes=64)
+        token_codes = [
+            reuse("token_codes_long", [P, CUT], U32, LAST_AT + 4 * C),
+            reuse("token_codes_short", [P, T - CUT], U32, LAST_AT - 8 * C),
+        ]
         slot_scales = keep.tile([P, S], U8, name="slot_scales", align_bytes=64)
         token_scales = keep.tile([P, T], U8, name="token_scales", align_bytes=64)
         words = keep.tile([P, E + 1, 2 * N], U8, name="words", align_bytes=64)
         scales = keep.tile([P, E + 1, N], U8, name="scales", align_bytes=64)
         bias = keep.tile([P, HALVES, BIAS_ROW], F32, name="bias")
         gates = keep.tile([P, 2, T], F32, name="gates")
-        y = [reuse("y0", [P, S], F32, 0), keep.tile([P, S], F32, name="y1")]
+        y = [reuse("y0", [P, S], F32, 8 * EARLY), keep.tile([P, S], F32, name="y1")]
         first = [keep.tile([P, T], F32, name=f"first{h}") for h in range(HALVES)]
         second = [keep.tile([P, T], F32, name=f"second{h}") for h in range(HALVES)]
-        base = reuse("base", [P, T], F32, woven_at[0])
+        base = reuse("base", [P, T], F32, 0)
         turned = keep.tile([P, T], F32, name="turned")
         partial = keep.tile([P, T], F32, name="partial")
         identity = keep.tile([P, P], F32, name="identity")
@@ -89,7 +93,8 @@ def tile_moe_shr_lin_bias_kernel(tc, xT, w_words, w_scales, b, gate, offs, pos1,
         nc.vector.memset(scales[:].rearrange("p e n -> p (e n)").bitcast(I32), 0)
         for u in range(2):
             nc.gpsimd.memset(pairs[:, u, T : WINDOWS[u]], 0)
-        nc.gpsimd.memset(rows[:, :, T:ROW_WINDOW], 0)
+        for i in range(2):
+            nc.gpsimd.memset(rows[i][:, T:ROW_WINDOW], 0)
         make_identity(nc, identity[:])
 
         w_scales_i = w_scales.bitcast(I32)
@@ -110,8 +115,16 @@ def tile_moe_shr_lin_bias_kernel(tc, xT, w_words, w_scales, b, gate, offs, pos1,
                 x_raw[:, u, :, lo:hi].rearrange("p i t -> p t i"),
             )
 
+        def picked(lo, hi):
+            return early[:, :, lo:hi] if hi <= EARLY else late[:, :, lo - EARLY : hi - EARLY]
+
         def gather(u, lo, hi):
-            nc.vector.tensor_copy(picked[:, u, lo:hi], pairs[:, u, 0 : WINDOWS[u]].indirect(offs_sb[:, lo // 16 : hi // 16]))
+            nc.vector.tensor_copy(picked(lo, hi)[:, u, :], pairs[:, u, 0 : WINDOWS[u]].indirect(offs_sb[:, lo // 16 : hi // 16]))
+
+        def woven(lo, hi):
+            if hi <= S - 2 * C:
+                return slot_x[:, 2 * lo : 2 * hi]
+            return third_x[:] if hi <= S - C else last_x[:]
 
         def weave(engine_copy, dst, planes):
             engine_copy(dst.rearrange("p (c u) -> p c u", u=2), planes.rearrange("p u c -> p c u"))
@@ -155,34 +168,32 @@ def tile_moe_shr_lin_bias_kernel(tc, xT, w_words, w_scales, b, gate, offs, pos1,
 
         round_pairs(nc.vector.tensor_copy, 0, 0, CUT)
         round_pairs(nc.scalar.copy, 0, CUT, T)
-        nc.scalar.copy(rows[:, :, 0:T], x_raw[:, 0])
-        round_pairs(nc.gpsimd.tensor_copy, 1, 0, T // 2)
-        round_pairs(nc.scalar.copy, 1, T // 2, T)
-        late = picked[:, 0, S - BY_SCALAR : S].bitcast(BF16).rearrange("p (c i) -> p i c", i=2)
+        nc.vector.tensor_copy(rows[0][:, 0:T], x_raw[:, 0, 0])
+        nc.scalar.copy(rows[1][:, 0:T], x_raw[:, 0, 1])
+        round_pairs(nc.gpsimd.tensor_copy, 1, 0, 160)
+        round_pairs(nc.scalar.copy, 1, 160, T)
+        halves = picked(S - BY_SCALAR, S)[:, 0, :].bitcast(BF16).rearrange("p (c i) -> p i c", i=2)
         for i in range(2):
-            nc.scalar.activation(late[:, i, :], rows[:, i, :].indirect(offs_sb[:, (S - BY_SCALAR) // 16 : S // 16]), COPY)
-        weave(nc.gpsimd.tensor_copy, token_x[:], pairs[:, :, 0:T])
+            nc.scalar.activation(halves[:, i, :], rows[i][:].indirect(offs_sb[:, (S - BY_SCALAR) // 16 : S // 16]), COPY)
 
-        gather(0, 0, S - BY_SCALAR)
-        for lo, hi in PIECES:
+        weave(nc.gpsimd.tensor_copy, token_x[:], pairs[:, :, 0:T])
+        gather(0, 0, EARLY)
+        gather(0, EARLY, S - BY_SCALAR)
+        for lo, hi in BY_GPSIMD + SCALAR_WEAVES:
             gather(1, lo, hi)
-        for j, (lo, hi) in enumerate(PIECES):
-            weave(nc.scalar.copy if j else nc.gpsimd.tensor_copy, slot_x[j][:], picked[:, :, lo:hi])
-        for j, (lo, hi) in enumerate(PIECES):
-            quantize(slot_codes(lo, hi), slot_scales[:, lo:hi], slot_x[j][:])
-            for e in range(lo // C, hi // C):
-                multiply(y0_ps[e][:], e, 0, slot_codes(e * C, (e + 1) * C), slot_scales[:, slots(e)])
+        for lo, hi in BY_GPSIMD:
+            weave(nc.gpsimd.tensor_copy, woven(lo, hi), picked(lo, hi))
+        for lo, hi in SCALAR_WEAVES:
+            weave(nc.scalar.copy, woven(lo, hi), picked(lo, hi))
+        for e in range(E):
+            lo, hi = e * C, (e + 1) * C
+            quantize(slot_codes(lo, hi), slot_scales[:, lo:hi], woven(lo, hi))
+            multiply(y0_ps[e][:], e, 0, slot_codes(lo, hi), slot_scales[:, lo:hi])
         for e in range(E):
             empty(y0_ps[e][:], e, 0)
 
-        token_codes = [
-            reuse("token_codes_long", [P, CUT], U32, woven_at[3]),
-            reuse("token_codes_short", [P, T - CUT], U32, woven_at[2]),
-        ]
         ys_ps = [bank(6, "ys_ps0", T), bank(0, "ys_ps1", T)]
         short_first = list(zip(token_codes, PARTS))[::-1]
-
-
         for codes, (lo, hi) in short_first:
             quantize(codes[:], token_scales[:, lo:hi], token_x[:, 2 * lo : 2 * hi])
         for codes, (lo, hi) in short_first:

@@ -23,16 +23,17 @@ ADD, MULT = mybir.AluOpType.add, mybir.AluOpType.mult
 IDENTITY = mybir.ActivationFunctionType.Identity
 COPY = mybir.ActivationFunctionType.Copy
 
-WINDOWS = (512, 512)
+WINDOWS = (640, 512)
 ROW_WINDOW = 512
 PIECES = ((0, 2 * C), (2 * C, 4 * C), (4 * C, 5 * C), (5 * C, S))
 BY_SCALAR = 320
-EARLY = 2 * C
-BY_GPSIMD = ((0, EARLY),)
-SCALAR_WEAVES = PIECES[1:]
+EARLY = S - BY_SCALAR
+BY_GPSIMD = ((0, 2 * C),)
+SCALAR_WEAVES = ((2 * C, EARLY), (EARLY, 4 * C), (4 * C, 5 * C), (5 * C, S))
+GATHERS = ((0, 2 * C), (2 * C, EARLY), (EARLY, 5 * C), (5 * C, S))
 CUT = 2 * P
 PARTS = ((0, CUT), (CUT, T))
-LAST_AT = 8 * S + 8 * C
+LAST_AT = 8 * EARLY + 4 * S + 8 * C
 BIAS_ROW = 8
 
 
@@ -178,8 +179,7 @@ def tile_moe_shr_lin_bias_kernel(tc, xT, w_words, w_scales, b, gate, offs, pos1,
 
         weave(nc.gpsimd.tensor_copy, token_x[:], pairs[:, :, 0:T])
         gather(0, 0, EARLY)
-        gather(0, EARLY, S - BY_SCALAR)
-        for lo, hi in BY_GPSIMD + SCALAR_WEAVES:
+        for lo, hi in GATHERS:
             gather(1, lo, hi)
         for lo, hi in BY_GPSIMD:
             weave(nc.gpsimd.tensor_copy, woven(lo, hi), picked(lo, hi))
@@ -222,8 +222,7 @@ def tile_moe_shr_lin_bias_kernel(tc, xT, w_words, w_scales, b, gate, offs, pos1,
         fetch(first[0], 0, 0, 0, T)
         for j in range(BLOCKS):
             turn(sums[j][:], first[0][:, block(j)], True, False)
-        for lo, hi in PARTS:
-            fetch(second[0], 0, 1, lo, hi)
+        fetch(second[0], 0, 1, 0, T)
         for j in range(BLOCKS):
             turn(sums[j][:], second[0][:, block(j)], False, True)
         for j in range(BLOCKS):

@@ -196,6 +196,10 @@ def tile_moe_shr_lin_bias_kernel(tc, xT, w_words, w_scales, b, gate, offs, pos1,
         short_first = list(zip(token_codes, PARTS))[::-1]
         for codes, (lo, hi) in short_first:
             quantize(codes[:], token_scales[:, lo:hi], token_x[:, 2 * lo : 2 * hi])
+
+        y1_ps = [bank(2 + j, f"y1_ps{j}", 2 * C) for j in range(E // 2)]
+        for e in range(E):
+            multiply(y1_ps[e // 2][:, slots(e % 2)], e, 1, slot_codes(e * C, (e + 1) * C), slot_scales[:, slots(e)])
         for codes, (lo, hi) in short_first:
             for at in range(lo, hi, P):
                 nc.tensor.matmul_mx(
@@ -207,18 +211,14 @@ def tile_moe_shr_lin_bias_kernel(tc, xT, w_words, w_scales, b, gate, offs, pos1,
                     start=True,
                     stop=True,
                 )
-
-        y1_ps = [bank(3 + j, f"y1_ps{j}", 2 * C) for j in range(E // 2)]
-        for e in range(E):
-            multiply(y1_ps[e // 2][:, slots(e % 2)], e, 1, slot_codes(e * C, (e + 1) * C), slot_scales[:, slots(e)])
         for e in range(E):
             empty(y1_ps[e // 2][:, slots(e % 2)], e, 1)
         for codes, (lo, hi) in short_first:
             multiply(ys_ps[1][:, lo:hi], E, 1, codes[:], token_scales[:, lo:hi])
         nc.scalar.copy(base[:], ys_ps[0][:])
 
-        sums = [bank(number, f"sum{j}", P) for j, number in enumerate((7, 1, 2))]
-        back = [bank(number, f"back{j}", P) for j, number in enumerate((3, 4, 6))]
+        sums = [bank(number, f"sum{j}", P) for j, number in enumerate((7, 1, 5))]
+        back = [bank(number, f"back{j}", P) for j, number in enumerate((2, 3, 6))]
         fetch(first[0], 0, 0, 0, T)
         for j in range(BLOCKS):
             turn(sums[j][:], first[0][:, block(j)], True, False)

@@ -23,14 +23,14 @@ ADD, MULT = mybir.AluOpType.add, mybir.AluOpType.mult
 IDENTITY = mybir.ActivationFunctionType.Identity
 COPY = mybir.ActivationFunctionType.Copy
 
-WINDOWS = (640, 512)
+WINDOWS = (704, 512)
 ROW_WINDOW = 512
 PIECES = ((0, 2 * C), (2 * C, 4 * C), (4 * C, 5 * C), (5 * C, S))
-BY_SCALAR = 320
+BY_SCALAR = 2 * C
 EARLY = S - BY_SCALAR
 BY_GPSIMD = ((0, 2 * C),)
-SCALAR_WEAVES = ((2 * C, EARLY), (EARLY, 4 * C), (4 * C, 5 * C), (5 * C, S))
-GATHERS = ((0, 2 * C), (2 * C, EARLY), (EARLY, 5 * C), (5 * C, S))
+SCALAR_WEAVES = ((2 * C, EARLY), (EARLY, 5 * C), (5 * C, S))
+GATHERS = BY_GPSIMD + SCALAR_WEAVES
 CUT = 2 * P
 PARTS = ((0, CUT), (CUT, T))
 LAST_AT = 8 * EARLY + 4 * S + 8 * C
@@ -171,8 +171,8 @@ def tile_moe_shr_lin_bias_kernel(tc, xT, w_words, w_scales, b, gate, offs, pos1,
         round_pairs(nc.scalar.copy, 0, CUT, T)
         nc.vector.tensor_copy(rows[0][:, 0:T], x_raw[:, 0, 0])
         nc.scalar.copy(rows[1][:, 0:T], x_raw[:, 0, 1])
-        round_pairs(nc.gpsimd.tensor_copy, 1, 0, 160)
-        round_pairs(nc.scalar.copy, 1, 160, T)
+        round_pairs(nc.gpsimd.tensor_copy, 1, 0, 192)
+        round_pairs(nc.scalar.copy, 1, 192, T)
         halves = picked(S - BY_SCALAR, S)[:, 0, :].bitcast(BF16).rearrange("p (c i) -> p i c", i=2)
         for i in range(2):
             nc.scalar.activation(halves[:, i, :], rows[i][:].indirect(offs_sb[:, (S - BY_SCALAR) // 16 : S // 16]), COPY)

@@ -23,14 +23,14 @@ ADD, MULT = mybir.AluOpType.add, mybir.AluOpType.mult
 IDENTITY = mybir.ActivationFunctionType.Identity
 COPY = mybir.ActivationFunctionType.Copy
 
-WINDOWS = (704, 512)
+WINDOWS = (640, 512)
 ROW_WINDOW = 512
 PIECES = ((0, 2 * C), (2 * C, 4 * C), (4 * C, 5 * C), (5 * C, S))
-BY_SCALAR = 2 * C
+BY_SCALAR = 288
 EARLY = S - BY_SCALAR
 BY_GPSIMD = ((0, 2 * C),)
-SCALAR_WEAVES = ((2 * C, EARLY), (EARLY, 5 * C), (5 * C, S))
-GATHERS = BY_GPSIMD + SCALAR_WEAVES
+SCALAR_WEAVES = ((2 * C, EARLY), (EARLY, 4 * C), (4 * C, 5 * C), (5 * C, S))
+GATHERS = ((0, 2 * C), (2 * C, EARLY), (EARLY, 5 * C), (5 * C, S))
 CUT = 2 * P
 PARTS = ((0, CUT), (CUT, T))
 LAST_AT = 8 * EARLY + 4 * S + 8 * C

@@ -79,8 +79,11 @@ def tile_moe_shr_lin_bias_kernel(tc, xT, w_words, w_scales, b, gate, offs, pos1,
         y = [reuse("y0", [P, S], F32, 8 * EARLY), keep.tile([P, S], F32, name="y1")]
         first = [keep.tile([P, T], F32, name=f"first{h}") for h in range(HALVES)]
         second = [keep.tile([P, T], F32, name=f"second{h}") for h in range(HALVES)]
-        base = reuse("base", [P, T], F32, 0)
+        base = reuse("base", [P, T + P], F32, 0)
         turned = keep.tile([P, T], F32, name="turned")
+        gate_column = keep.tile([P, 1], F32, name="gate_column")
+        plain = keep.tile([P, P], F32, name="plain")
+        gated = keep.tile([P, P], F32, name="gated")
         partial = keep.tile([P, T], F32, name="partial")
         identity = keep.tile([P, P], F32, name="identity")
         result = [keep.tile([P, T], F32, name=f"result{h}") for h in range(HALVES)]
@@ -109,6 +112,9 @@ def tile_moe_shr_lin_bias_kernel(tc, xT, w_words, w_scales, b, gate, offs, pos1,
         nc.sync.dma_start(pos1_sb[:], pos1)
         nc.sync.dma_start(pos2_sb[:], pos2)
         nc.sync.dma_start(out=gates[:], in_=gate[:, 0:P, :].rearrange("g p t -> p g t"))
+
+        with nc.allow_non_contiguous_dma(reason="one gate a partition"):
+            nc.sync.dma_start(out=gate_column[:], in_=gate[1, 0, CUT:T].rearrange("(p j) -> p j", j=1))
 
         def round_pairs(engine_copy, u, lo, hi):
             engine_copy(
@@ -192,7 +198,8 @@ def tile_moe_shr_lin_bias_kernel(tc, xT, w_words, w_scales, b, gate, offs, pos1,
         for e in range(E):
             empty(y0_ps[e][:], e, 0)
 
-        ys_ps = [bank(6, "ys_ps0", T), bank(0, "ys_ps1", T)]
+        ys_turned = bank(5, "ys_turned", T + P)
+        ys_long = bank(0, "ys_long", CUT)
         short_first = list(zip(token_codes, PARTS))[::-1]
         for codes, (lo, hi) in short_first:
             quantize(codes[:], token_scales[:, lo:hi], token_x[:, 2 * lo : 2 * hi])
@@ -200,25 +207,37 @@ def tile_moe_shr_lin_bias_kernel(tc, xT, w_words, w_scales, b, gate, offs, pos1,
         y1_ps = [bank(2 + j, f"y1_ps{j}", 2 * C) for j in range(E // 2)]
         for e in range(E):
             multiply(y1_ps[e // 2][:, slots(e % 2)], e, 1, slot_codes(e * C, (e + 1) * C), slot_scales[:, slots(e)])
+
+        def multiply_turned(acc, h, codes, code_scales):
+            nc.tensor.matmul_mx(
+                out=acc,
+                lhsT=codes.bitcast(E4M3X4),
+                lhsT_scale=code_scales,
+                rhs=words[:, E, 2 * P * h : 2 * P * (h + 1)].bitcast(E2M1X4),
+                rhs_scale=scales[:, E, P * h : P * (h + 1)],
+                start=True,
+                stop=True,
+            )
+
+        multiply_turned(ys_turned[:, T : T + P], 1, token_codes[1][:], token_scales[:, CUT:T])
         for codes, (lo, hi) in short_first:
             for at in range(lo, hi, P):
-                nc.tensor.matmul_mx(
-                    out=ys_ps[0][:, at : at + P],
-                    lhsT=codes[:, at - lo : at - lo + P].bitcast(E4M3X4),
-                    lhsT_scale=token_scales[:, at : at + P],
-                    rhs=words[:, E, 0 : 2 * P].bitcast(E2M1X4),
-                    rhs_scale=scales[:, E, 0:P],
-                    start=True,
-                    stop=True,
-                )
+                multiply_turned(ys_turned[:, at : at + P], 0, codes[:, at - lo : at - lo + P], token_scales[:, at : at + P])
         for e in range(E):
             empty(y1_ps[e // 2][:, slots(e % 2)], e, 1)
-        for codes, (lo, hi) in short_first:
-            multiply(ys_ps[1][:, lo:hi], E, 1, codes[:], token_scales[:, lo:hi])
-        nc.scalar.copy(base[:], ys_ps[0][:])
+        multiply(ys_long[:], E, 1, token_codes[0][:], token_scales[:, 0:CUT])
 
-        sums = [bank(number, f"sum{j}", P) for j, number in enumerate((7, 1, 5))]
-        back = [bank(number, f"back{j}", P) for j, number in enumerate((2, 3, 6))]
+        nc.scalar.activation(plain[:], y[1][:].indirect(pos2_sb[:, CUT // 16 : T // 16]), COPY)
+        nc.scalar.copy(base[:], ys_turned[:])
+        across = bank(4, "across", P)
+        turn(across[:], plain[:], True, True)
+        nc.scalar.activation(gated[:], across[:], COPY, scale=gate_column[:])
+        last = bank(4, "last", P)
+        turn(last[:], base[:, T : T + P], True, False)
+        turn(last[:], gated[:], False, True)
+
+        sums = [bank(number, f"sum{j}", P) for j, number in enumerate((7, 1, 6))]
+        back = [bank(number, f"back{j}", P) for j, number in enumerate((2, 3, 5))]
         fetch(first[0], 0, 0, 0, T)
         for j in range(BLOCKS):
             turn(sums[j][:], first[0][:, block(j)], True, False)
@@ -236,10 +255,11 @@ def tile_moe_shr_lin_bias_kernel(tc, xT, w_words, w_scales, b, gate, offs, pos1,
                 nc.scalar.activation(result[0][:, block(j)], back[j][:], IDENTITY, bias=bias[:, 0, E : E + 1])
             nc.scalar.dma_start(out=out[0:P, lo:hi], in_=result[0][:, lo:hi])
 
-        fetch(first[1], 1, 0, 0, T)
         fetch(second[1], 1, 1, 0, CUT)
-        nc.vector.scalar_tensor_tensor(partial[:], ys_ps[1][:], bias[:, 1, E : E + 1], first[1][:], ADD, ADD)
-        fetch(second[1], 1, 1, CUT, T)
-        for lo, hi in PARTS:
-            nc.vector.tensor_tensor(result[1][:, lo:hi], partial[:, lo:hi], second[1][:, lo:hi], ADD)
-            nc.sync.dma_start(out=out[P:N, lo:hi], in_=result[1][:, lo:hi])
+        fetch(first[1], 1, 0, 0, CUT)
+        nc.vector.scalar_tensor_tensor(partial[:, 0:CUT], ys_long[:], bias[:, 1, E : E + 1], second[1][:, 0:CUT], ADD, ADD)
+        fetch(first[1], 1, 0, CUT, T)
+        nc.vector.tensor_tensor(result[1][:, 0:CUT], partial[:, 0:CUT], first[1][:, 0:CUT], ADD)
+        nc.sync.dma_start(out=out[P:N, 0:CUT], in_=result[1][:, 0:CUT])
+        nc.vector.scalar_tensor_tensor(result[1][:, CUT:T], last[:], bias[:, 1, E : E + 1], first[1][:, CUT:T], ADD, ADD)
+        nc.sync.dma_start(out=out[P:N, CUT:T], in_=result[1][:, CUT:T])

@@ -241,7 +241,8 @@ def tile_moe_shr_lin_bias_kernel(tc, xT, w_words, w_scales, b, gate, offs, pos1,
         fetch(first[0], 0, 0, 0, T)
         for j in range(BLOCKS):
             turn(sums[j][:], first[0][:, block(j)], True, False)
-        fetch(second[0], 0, 1, 0, T)
+        for lo, hi in PARTS:
+            fetch(second[0], 0, 1, lo, hi)
         for j in range(BLOCKS):
             turn(sums[j][:], second[0][:, block(j)], False, True)
         for j in range(BLOCKS):

@@ -23,17 +23,14 @@ ADD, MULT = mybir.AluOpType.add, mybir.AluOpType.mult
 IDENTITY = mybir.ActivationFunctionType.Identity
 COPY = mybir.ActivationFunctionType.Copy
 
-WINDOWS = (640, 512)
-ROW_WINDOW = 512
-PIECES = ((0, 2 * C), (2 * C, 4 * C), (4 * C, 5 * C), (5 * C, S))
-BY_SCALAR = 288
-EARLY = S - BY_SCALAR
-BY_GPSIMD = ((0, 2 * C),)
-SCALAR_WEAVES = ((2 * C, EARLY), (EARLY, 4 * C), (4 * C, 5 * C), (5 * C, S))
-GATHERS = ((0, 2 * C), (2 * C, EARLY), (EARLY, 5 * C), (5 * C, S))
+WINDOW = 512
+DIRECT = 192
+MIDDLE = 3 * C
+ORDER = (2, 0, 1, 3, 4, 5)
 CUT = 2 * P
 PARTS = ((0, CUT), (CUT, T))
-LAST_AT = 8 * EARLY + 4 * S + 8 * C
+LATE_AT = 4 * (S - C)
+LAST_AT = LATE_AT + 4 * S + 8 * C
 BIAS_ROW = 8
 
 
@@ -55,16 +52,18 @@ def tile_moe_shr_lin_bias_kernel(tc, xT, w_words, w_scales, b, gate, offs, pos1,
         pos1_sb = lists.tile([P, T // 16], U16, name="pos1_sb")
         pos2_sb = lists.tile([P, T // 16], U16, name="pos2_sb")
 
-        x_raw = keep.tile([P, 2, 2, T], F32, name="x_raw")
-        pairs = keep.tile([P, 2, WINDOWS[0]], U32, name="pairs")
-        early = reuse("early", [P, 2, EARLY], U32, 0)
-        late = reuse("late", [P, 2, S - EARLY], U32, 8 * EARLY)
-        slot_x = keep.tile([P, 2 * (S - 2 * C)], U32, name="slot_x", align_bytes=64)
+        x_raw = [keep.tile([P, 2 * T], F32, name=f"x_raw{u}") for u in range(2)]
+        row3 = keep.tile([P, T], F32, name="row3")
+        row1 = keep.tile([P, WINDOW], BF16, name="row1")
+        pairs = keep.tile([P, 2, WINDOW], U32, name="pairs")
+        early = reuse("early", [P, 2, MIDDLE - DIRECT], U32, 0)
+        late = reuse("late", [P, 2, S - MIDDLE], U32, LATE_AT)
+        head_x = keep.tile([P, 4 * C], U32, name="head_x", align_bytes=64)
+        slot_x = [keep.tile([P, 2 * C], U32, name=f"slot_x{e}", align_bytes=64) for e in (2, 3)]
         third_x = reuse("third_x", [P, 2 * C], U32, LAST_AT - 8 * C)
         last_x = reuse("last_x", [P, 2 * C], U32, LAST_AT)
-        rows = [keep.tile([P, ROW_WINDOW], BF16, name=f"row{i}") for i in range(2)]
-        codes_first = keep.tile([P, 2 * C], U32, name="codes_first", align_bytes=64)
-        codes_rest = reuse("codes_rest", [P, S - 2 * C], U32, 0)
+        codes_first = keep.tile([P, C], U32, name="codes_first", align_bytes=64)
+        codes_rest = reuse("codes_rest", [P, S - C], U32, 0)
         token_x = keep.tile([P, 2 * T], U32, name="token_x", align_bytes=64)
         token_codes = [
             reuse("token_codes_long", [P, CUT], U32, LAST_AT + 4 * C),
@@ -76,7 +75,7 @@ def tile_moe_shr_lin_bias_kernel(tc, xT, w_words, w_scales, b, gate, offs, pos1,
         scales = keep.tile([P, E + 1, N], U8, name="scales", align_bytes=64)
         bias = keep.tile([P, HALVES, BIAS_ROW], F32, name="bias")
         gates = keep.tile([P, 2, T], F32, name="gates")
-        y = [reuse("y0", [P, S], F32, 8 * EARLY), keep.tile([P, S], F32, name="y1")]
+        y = [reuse("y0", [P, S], F32, LATE_AT), keep.tile([P, S], F32, name="y1")]
         first = [keep.tile([P, T], F32, name=f"first{h}") for h in range(HALVES)]
         second = [keep.tile([P, T], F32, name=f"second{h}") for h in range(HALVES)]
         base = reuse("base", [P, T + P], F32, 0)
@@ -90,15 +89,14 @@ def tile_moe_shr_lin_bias_kernel(tc, xT, w_words, w_scales, b, gate, offs, pos1,
         y0_ps = [bank(e, f"y0_ps{e}", C) for e in range(E)]
 
         x_view = xT.rearrange("(p u i) t -> p u i t", u=2, i=2)
-        nc.sync.dma_start(out=x_raw[:, 0], in_=x_view[:, 0])
+        nc.sync.dma_start(out=x_raw[0][:], in_=x_view[:, 0].rearrange("p i t -> p (i t)"))
         nc.sync.dma_start(offs_sb[:], offs)
-        nc.sync.dma_start(out=x_raw[:, 1], in_=x_view[:, 1])
+        nc.sync.dma_start(out=x_raw[1][:], in_=x_view[:, 1].rearrange("p i t -> p (i t)"))
+        nc.sync.dma_start(out=row3[:], in_=x_view[:, 1, 1])
 
         nc.vector.memset(scales[:].rearrange("p e n -> p (e n)").bitcast(I32), 0)
-        for u in range(2):
-            nc.gpsimd.memset(pairs[:, u, T : WINDOWS[u]], 0)
-        for i in range(2):
-            nc.gpsimd.memset(rows[i][:, T:ROW_WINDOW], 0)
+        nc.gpsimd.memset(pairs[:, :, T:WINDOW], 0)
+        nc.gpsimd.memset(row1[:, T:WINDOW], 0)
         make_identity(nc, identity[:])
 
         w_scales_i = w_scales.bitcast(I32)
@@ -119,19 +117,19 @@ def tile_moe_shr_lin_bias_kernel(tc, xT, w_words, w_scales, b, gate, offs, pos1,
         def round_pairs(engine_copy, u, lo, hi):
             engine_copy(
                 pairs[:, u, lo:hi].bitcast(BF16).rearrange("p (t i) -> p t i", i=2),
-                x_raw[:, u, :, lo:hi].rearrange("p i t -> p t i"),
+                x_raw[u][:].rearrange("p (i t) -> p t i", i=2)[:, lo:hi],
             )
 
         def picked(lo, hi):
-            return early[:, :, lo:hi] if hi <= EARLY else late[:, :, lo - EARLY : hi - EARLY]
+            return early[:, :, lo - DIRECT : hi - DIRECT] if hi <= MIDDLE else late[:, :, lo - MIDDLE : hi - MIDDLE]
 
         def gather(u, lo, hi):
-            nc.vector.tensor_copy(picked(lo, hi)[:, u, :], pairs[:, u, 0 : WINDOWS[u]].indirect(offs_sb[:, lo // 16 : hi // 16]))
+            nc.vector.tensor_copy(picked(lo, hi)[:, u, :], pairs[:, u, :].indirect(offs_sb[:, lo // 16 : hi // 16]))
 
         def woven(lo, hi):
-            if hi <= S - 2 * C:
-                return slot_x[:, 2 * lo : 2 * hi]
-            return third_x[:] if hi <= S - C else last_x[:]
+            if hi <= 2 * C:
+                return head_x[:, 2 * lo : 2 * hi]
+            return (slot_x + [third_x, last_x])[lo // C - 2][:]
 
         def weave(engine_copy, dst, planes):
             engine_copy(dst.rearrange("p (c u) -> p c u", u=2), planes.rearrange("p u c -> p c u"))
@@ -153,8 +151,8 @@ def tile_moe_shr_lin_bias_kernel(tc, xT, w_words, w_scales, b, gate, offs, pos1,
         def slots(e):
             return slice(e * C, (e + 1) * C)
 
-        def slot_codes(lo, hi):
-            return codes_first[:, lo:hi] if hi <= 2 * C else codes_rest[:, lo - 2 * C : hi - 2 * C]
+        def slot_codes(place):
+            return codes_first[:] if place == 0 else codes_rest[:, slots(place - 1)]
 
         def block(j):
             return slice(j * P, (j + 1) * P)
@@ -175,28 +173,27 @@ def tile_moe_shr_lin_bias_kernel(tc, xT, w_words, w_scales, b, gate, offs, pos1,
 
         round_pairs(nc.vector.tensor_copy, 0, 0, CUT)
         round_pairs(nc.scalar.copy, 0, CUT, T)
-        nc.vector.tensor_copy(rows[0][:, 0:T], x_raw[:, 0, 0])
-        nc.scalar.copy(rows[1][:, 0:T], x_raw[:, 0, 1])
-        round_pairs(nc.gpsimd.tensor_copy, 1, 0, 192)
-        round_pairs(nc.scalar.copy, 1, 192, T)
-        halves = picked(S - BY_SCALAR, S)[:, 0, :].bitcast(BF16).rearrange("p (c i) -> p i c", i=2)
-        for i in range(2):
-            nc.scalar.activation(halves[:, i, :], rows[i][:].indirect(offs_sb[:, (S - BY_SCALAR) // 16 : S // 16]), COPY)
+        nc.vector.tensor_copy(row1[:, 0:T], x_raw[0][:, T : 2 * T])
+        round_pairs(nc.gpsimd.tensor_copy, 1, 0, T)
+        direct = head_x[:, 0 : 2 * DIRECT].bitcast(BF16).rearrange("p (c d) -> p d c", d=4)
+        for d, window in ((0, x_raw[0]), (2, x_raw[1]), (1, row1), (3, row3)):
+            nc.scalar.activation(direct[:, d, :], window[:].indirect(offs_sb[:, 0 : DIRECT // 16]), COPY)
 
         weave(nc.gpsimd.tensor_copy, token_x[:], pairs[:, :, 0:T])
-        gather(0, 0, EARLY)
-        for lo, hi in GATHERS:
-            gather(1, lo, hi)
-        for lo, hi in BY_GPSIMD:
-            weave(nc.gpsimd.tensor_copy, woven(lo, hi), picked(lo, hi))
-        for lo, hi in SCALAR_WEAVES:
-            weave(nc.scalar.copy, woven(lo, hi), picked(lo, hi))
-        for e in range(E):
-            lo, hi = e * C, (e + 1) * C
-            quantize(slot_codes(lo, hi), slot_scales[:, lo:hi], woven(lo, hi))
-            multiply(y0_ps[e][:], e, 0, slot_codes(lo, hi), slot_scales[:, lo:hi])
-        for e in range(E):
-            empty(y0_ps[e][:], e, 0)
+        gather(0, DIRECT, MIDDLE)
+        gather(0, MIDDLE, S)
+        gather(1, DIRECT, MIDDLE)
+        for e in range(MIDDLE // C, E):
+            gather(1, e * C, (e + 1) * C)
+        weave(nc.gpsimd.tensor_copy, woven(2 * C, MIDDLE), picked(2 * C, MIDDLE))
+        weave(nc.scalar.copy, woven(DIRECT, 2 * C), picked(DIRECT, 2 * C))
+        for e in range(MIDDLE // C, E):
+            weave(nc.scalar.copy, woven(e * C, (e + 1) * C), picked(e * C, (e + 1) * C))
+        for place, e in enumerate(ORDER):
+            quantize(slot_codes(place), slot_scales[:, slots(e)], woven(e * C, (e + 1) * C))
+            multiply(y0_ps[place][:], e, 0, slot_codes(place), slot_scales[:, slots(e)])
+        for place, e in enumerate(ORDER):
+            empty(y0_ps[place][:], e, 0)
 
         ys_turned = bank(5, "ys_turned", T + P)
         ys_long = bank(0, "ys_long", CUT)
@@ -205,8 +202,8 @@ def tile_moe_shr_lin_bias_kernel(tc, xT, w_words, w_scales, b, gate, offs, pos1,
             quantize(codes[:], token_scales[:, lo:hi], token_x[:, 2 * lo : 2 * hi])
 
         y1_ps = [bank(2 + j, f"y1_ps{j}", 2 * C) for j in range(E // 2)]
-        for e in range(E):
-            multiply(y1_ps[e // 2][:, slots(e % 2)], e, 1, slot_codes(e * C, (e + 1) * C), slot_scales[:, slots(e)])
+        for place, e in enumerate(ORDER):
+            multiply(y1_ps[place // 2][:, slots(place % 2)], e, 1, slot_codes(place), slot_scales[:, slots(e)])
 
         def multiply_turned(acc, h, codes, code_scales):
             nc.tensor.matmul_mx(
@@ -223,19 +220,12 @@ def tile_moe_shr_lin_bias_kernel(tc, xT, w_words, w_scales, b, gate, offs, pos1,
         for codes, (lo, hi) in short_first:
             for at in range(lo, hi, P):
                 multiply_turned(ys_turned[:, at : at + P], 0, codes[:, at - lo : at - lo + P], token_scales[:, at : at + P])
-        for e in range(E):
-            empty(y1_ps[e // 2][:, slots(e % 2)], e, 1)
+        for place, e in enumerate(ORDER):
+            empty(y1_ps[place // 2][:, slots(place % 2)], e, 1)
         multiply(ys_long[:], E, 1, token_codes[0][:], token_scales[:, 0:CUT])
 
         nc.scalar.activation(plain[:], y[1][:].indirect(pos2_sb[:, CUT // 16 : T // 16]), COPY)
         nc.scalar.copy(base[:], ys_turned[:])
-        across = bank(4, "across", P)
-        turn(across[:], plain[:], True, True)
-        nc.scalar.activation(gated[:], across[:], COPY, scale=gate_column[:])
-        last = bank(4, "last", P)
-        turn(last[:], base[:, T : T + P], True, False)
-        turn(last[:], gated[:], False, True)
-
         sums = [bank(number, f"sum{j}", P) for j, number in enumerate((7, 1, 6))]
         back = [bank(number, f"back{j}", P) for j, number in enumerate((2, 3, 5))]
         fetch(first[0], 0, 0, 0, T)
@@ -249,6 +239,12 @@ def tile_moe_shr_lin_bias_kernel(tc, xT, w_words, w_scales, b, gate, offs, pos1,
             turn(back[j][:], base[:, block(j)], True, False)
         for j in range(BLOCKS):
             nc.scalar.copy(turned[:, block(j)], sums[j][:])
+        across = bank(7, "across", P)
+        turn(across[:], plain[:], True, True)
+        nc.scalar.activation(gated[:], across[:], COPY, scale=gate_column[:])
+        last = bank(4, "last", P)
+        turn(last[:], base[:, T : T + P], True, False)
+        turn(last[:], gated[:], False, True)
         for j in range(BLOCKS):
             turn(back[j][:], turned[:, block(j)], False, True)
         for lo, hi in PARTS:

@@ -105,11 +105,14 @@ def tile_moe_shr_lin_bias_kernel(tc, xT, w_words, w_scales, b, gate, offs, pos1,
                 out=scales[32 * quadrant : 32 * quadrant + 4].bitcast(I32),
                 in_=w_scales_i[:, 0, 4 * quadrant : 4 * quadrant + 4, :].rearrange("e q n -> q e n"),
             )
-        nc.sync.dma_start(out=words[:].bitcast(I32), in_=w_words.bitcast(I32).rearrange("e a p x -> p (e a) x"))
+        words_i = w_words.bitcast(I32).rearrange("e a p x -> p (e a) x")
+        for lo, hi in ((0, E // 2), (E // 2, E + 1)):
+            nc.sync.dma_start(out=words[:, lo:hi].bitcast(I32), in_=words_i[:, lo:hi])
         nc.sync.dma_start(out=bias[:, :, 0 : E + 1], in_=b.rearrange("(h p) e -> p h e", p=P))
         nc.sync.dma_start(pos1_sb[:], pos1)
         nc.sync.dma_start(pos2_sb[:], pos2)
-        nc.sync.dma_start(out=gates[:], in_=gate[:, 0:P, :].rearrange("g p t -> p g t"))
+        for g in range(2):
+            nc.sync.dma_start(out=gates[:, g], in_=gate[g, 0:P, :])
 
         with nc.allow_non_contiguous_dma(reason="one gate a partition"):
             nc.sync.dma_start(out=gate_column[:], in_=gate[1, 0, CUT:T].rearrange("(p j) -> p j", j=1))
@@ -239,10 +242,10 @@ def tile_moe_shr_lin_bias_kernel(tc, xT, w_words, w_scales, b, gate, offs, pos1,
             turn(back[j][:], base[:, block(j)], True, False)
         for j in range(BLOCKS):
             nc.scalar.copy(turned[:, block(j)], sums[j][:])
-        across = bank(7, "across", P)
+        across = bank(4, "across", P)
         turn(across[:], plain[:], True, True)
         nc.scalar.activation(gated[:], across[:], COPY, scale=gate_column[:])
-        last = bank(4, "last", P)
+        last = bank(7, "last", P)
         turn(last[:], base[:, T : T + P], True, False)
         turn(last[:], gated[:], False, True)
         for j in range(BLOCKS):

@@ -81,6 +81,7 @@ def tile_moe_shr_lin_bias_kernel(tc, xT, w_words, w_scales, b, gate, offs, pos1,
         base = reuse("base", [P, T + P], F32, 0)
         turned = keep.tile([P, T], F32, name="turned")
         gate_column = keep.tile([P, 1], F32, name="gate_column")
+        diagonal = keep.tile([P, P], F32, name="diagonal")
         plain = keep.tile([P, P], F32, name="plain")
         gated = keep.tile([P, P], F32, name="gated")
         partial = keep.tile([P, T], F32, name="partial")
@@ -105,17 +106,11 @@ def tile_moe_shr_lin_bias_kernel(tc, xT, w_words, w_scales, b, gate, offs, pos1,
                 out=scales[32 * quadrant : 32 * quadrant + 4].bitcast(I32),
                 in_=w_scales_i[:, 0, 4 * quadrant : 4 * quadrant + 4, :].rearrange("e q n -> q e n"),
             )
-        words_i = w_words.bitcast(I32).rearrange("e a p x -> p (e a) x")
-        for lo, hi in ((0, E // 2), (E // 2, E + 1)):
-            nc.sync.dma_start(out=words[:, lo:hi].bitcast(I32), in_=words_i[:, lo:hi])
+        nc.sync.dma_start(out=words[:].bitcast(I32), in_=w_words.bitcast(I32).rearrange("e a p x -> p (e a) x"))
         nc.sync.dma_start(out=bias[:, :, 0 : E + 1], in_=b.rearrange("(h p) e -> p h e", p=P))
         nc.sync.dma_start(pos1_sb[:], pos1)
         nc.sync.dma_start(pos2_sb[:], pos2)
-        for g in range(2):
-            nc.sync.dma_start(out=gates[:, g], in_=gate[g, 0:P, :])
-
-        with nc.allow_non_contiguous_dma(reason="one gate a partition"):
-            nc.sync.dma_start(out=gate_column[:], in_=gate[1, 0, CUT:T].rearrange("(p j) -> p j", j=1))
+        nc.sync.dma_start(out=gates[:], in_=gate[:, 0:P, :].rearrange("g p t -> p g t"))
 
         def round_pairs(engine_copy, u, lo, hi):
             engine_copy(
@@ -203,6 +198,8 @@ def tile_moe_shr_lin_bias_kernel(tc, xT, w_words, w_scales, b, gate, offs, pos1,
         short_first = list(zip(token_codes, PARTS))[::-1]
         for codes, (lo, hi) in short_first:
             quantize(codes[:], token_scales[:, lo:hi], token_x[:, 2 * lo : 2 * hi])
+
+        nc.vector.scalar_tensor_tensor(diagonal[:], gates[:, 1, CUT:T], 1.0, identity[:], MULT, MULT, accum_out=gate_column[:])
 
         y1_ps = [bank(2 + j, f"y1_ps{j}", 2 * C) for j in range(E // 2)]
         for place, e in enumerate(ORDER):

@@ -242,11 +242,11 @@ def tile_moe_shr_lin_bias_kernel(tc, xT, w_words, w_scales, b, gate, offs, pos1,
         across = bank(4, "across", P)
         turn(across[:], plain[:], True, True)
         nc.scalar.activation(gated[:], across[:], COPY, scale=gate_column[:])
-        last = bank(7, "last", P)
-        turn(last[:], base[:, T : T + P], True, False)
-        turn(last[:], gated[:], False, True)
         for j in range(BLOCKS):
             turn(back[j][:], turned[:, block(j)], False, True)
+        last = bank(6, "last", P)
+        turn(last[:], base[:, T : T + P], True, False)
+        turn(last[:], gated[:], False, True)
         for lo, hi in PARTS:
             for j in range(lo // P, hi // P):
                 nc.scalar.activation(result[0][:, block(j)], back[j][:], IDENTITY, bias=bias[:, 0, E : E + 1])

@@ -183,8 +183,9 @@ def tile_moe_shr_lin_bias_kernel(tc, xT, w_words, w_scales, b, gate, offs, pos1,
         gather(1, DIRECT, MIDDLE)
         for e in range(MIDDLE // C, E):
             gather(1, e * C, (e + 1) * C)
-        weave(nc.gpsimd.tensor_copy, woven(2 * C, MIDDLE), picked(2 * C, MIDDLE))
+        weave(nc.gpsimd.tensor_copy, slot_x[0][:, C : 2 * C], picked(MIDDLE - C // 2, MIDDLE))
         weave(nc.scalar.copy, woven(DIRECT, 2 * C), picked(DIRECT, 2 * C))
+        weave(nc.scalar.copy, slot_x[0][:, 0:C], picked(2 * C, MIDDLE - C // 2))
         for e in range(MIDDLE // C, E):
             weave(nc.scalar.copy, woven(e * C, (e + 1) * C), picked(e * C, (e + 1) * C))
         for place, e in enumerate(ORDER):

from contextlib import ExitStack

import concourse.mybir as mybir
from concourse.masks import make_identity

K, T, E, C, N = 512, 384, 6, 128, 256
S = E * C
P = 128
HALVES = N // P
BLOCKS = T // P
FLOPS = 2 * K * N * (S + T)

F32 = mybir.dt.float32
BF16 = mybir.dt.bfloat16
I32 = mybir.dt.int32
U32 = mybir.dt.uint32
U16 = mybir.dt.uint16
U8 = mybir.dt.uint8
E4M3X4 = mybir.dt.float8_e4m3fn_x4
E2M1X4 = mybir.dt.float4_e2m1fn_x4

ADD, MULT = mybir.AluOpType.add, mybir.AluOpType.mult
IDENTITY = mybir.ActivationFunctionType.Identity
COPY = mybir.ActivationFunctionType.Copy

WINDOW = 512
DIRECT = 192
MIDDLE = 3 * C
ORDER = (2, 0, 1, 3, 4, 5)
CUT = 2 * P
PARTS = ((0, CUT), (CUT, T))
LATE_AT = 4 * (S - C)
LAST_AT = LATE_AT + 4 * S + 8 * C
BIAS_ROW = 8


def tile_moe_shr_lin_bias_kernel(tc, xT, w_words, w_scales, b, gate, offs, pos1, pos2, out):
    nc = tc.nc
    with ExitStack() as ctx:
        lists = ctx.enter_context(tc.tile_pool(name="lists", bufs=1))
        keep = ctx.enter_context(tc.tile_pool(name="keep", bufs=1))
        reused = ctx.enter_context(tc.tile_pool(name="reused", bufs=1))
        psum = ctx.enter_context(tc.psum_pool(name="psum", bufs=1))

        def bank(number, name, columns):
            return psum.tile([P, columns], F32, name=name, tag=f"bank{number}")

        def reuse(name, shape, dtype, offset):
            return reused.tile(shape, dtype, name=name, align_bytes=64, offset=offset)

        offs_sb = lists.tile([P, S // 16], U16, name="offs_sb")
        pos1_sb = lists.tile([P, T // 16], U16, name="pos1_sb")
        pos2_sb = lists.tile([P, T // 16], U16, name="pos2_sb")

        x_raw = [keep.tile([P, 2 * T], F32, name=f"x_raw{u}") for u in range(2)]
        row3 = keep.tile([P, T], F32, name="row3")
        row1 = keep.tile([P, WINDOW], BF16, name="row1")
        pairs = keep.tile([P, 2, WINDOW], U32, name="pairs")
        early = reuse("early", [P, 2, MIDDLE - DIRECT], U32, 0)
        late = reuse("late", [P, 2, S - MIDDLE], U32, LATE_AT)
        head_x = keep.tile([P, 4 * C], U32, name="head_x", align_bytes=64)
        slot_x = [keep.tile([P, 2 * C], U32, name=f"slot_x{e}", align_bytes=64) for e in (2, 3)]
        third_x = reuse("third_x", [P, 2 * C], U32, LAST_AT - 8 * C)
        last_x = reuse("last_x", [P, 2 * C], U32, LAST_AT)
        codes_first = keep.tile([P, C], U32, name="codes_first", align_bytes=64)
        codes_rest = reuse("codes_rest", [P, S - C], U32, 0)
        token_x = keep.tile([P, 2 * T], U32, name="token_x", align_bytes=64)
        token_codes = [
            reuse("token_codes_long", [P, CUT], U32, LAST_AT + 4 * C),
            reuse("token_codes_short", [P, T - CUT], U32, LAST_AT - 8 * C),
        ]
        slot_scales = keep.tile([P, S], U8, name="slot_scales", align_bytes=64)
        token_scales = keep.tile([P, T], U8, name="token_scales", align_bytes=64)
        words = keep.tile([P, E + 1, 2 * N], U8, name="words", align_bytes=64)
        scales = keep.tile([P, E + 1, N], U8, name="scales", align_bytes=64)
        bias = keep.tile([P, HALVES, BIAS_ROW], F32, name="bias")
        gates = keep.tile([P, 2, T], F32, name="gates")
        y = [reuse("y0", [P, S], F32, LATE_AT), keep.tile([P, S], F32, name="y1")]
        first = [keep.tile([P, T], F32, name=f"first{h}") for h in range(HALVES)]
        second = [keep.tile([P, T], F32, name=f"second{h}") for h in range(HALVES)]
        base = reuse("base", [P, T + P], F32, 0)
        turned = keep.tile([P, T], F32, name="turned")
        gate_column = keep.tile([P, 1], F32, name="gate_column")
        diagonal = keep.tile([P, P], F32, name="diagonal")
        plain = keep.tile([P, P], F32, name="plain")
        gated = keep.tile([P, P], F32, name="gated")
        partial = keep.tile([P, T], F32, name="partial")
        identity = keep.tile([P, P], F32, name="identity")
        result = [keep.tile([P, T], F32, name=f"result{h}") for h in range(HALVES)]
        y0_ps = [bank(e, f"y0_ps{e}", C) for e in range(E)]

        x_view = xT.rearrange("(p u i) t -> p u i t", u=2, i=2)
        nc.sync.dma_start(out=x_raw[0][:], in_=x_view[:, 0].rearrange("p i t -> p (i t)"))
        nc.sync.dma_start(offs_sb[:], offs)
        nc.sync.dma_start(out=x_raw[1][:], in_=x_view[:, 1].rearrange("p i t -> p (i t)"))
        nc.sync.dma_start(out=row3[:], in_=x_view[:, 1, 1])

        nc.vector.memset(scales[:].rearrange("p e n -> p (e n)").bitcast(I32), 0)
        nc.gpsimd.memset(pairs[:, :, T:WINDOW], 0)
        nc.gpsimd.memset(row1[:, T:WINDOW], 0)
        make_identity(nc, identity[:])

        w_scales_i = w_scales.bitcast(I32)
        for quadrant in range(4):
            nc.sync.dma_start(
                out=scales[32 * quadrant : 32 * quadrant + 4].bitcast(I32),
                in_=w_scales_i[:, 0, 4 * quadrant : 4 * quadrant + 4, :].rearrange("e q n -> q e n"),
            )
        nc.sync.dma_start(out=words[:].bitcast(I32), in_=w_words.bitcast(I32).rearrange("e a p x -> p (e a) x"))
        nc.sync.dma_start(out=bias[:, :, 0 : E + 1], in_=b.rearrange("(h p) e -> p h e", p=P))
        nc.sync.dma_start(pos1_sb[:], pos1)
        nc.sync.dma_start(pos2_sb[:], pos2)
        nc.sync.dma_start(out=gates[:], in_=gate[:, 0:P, :].rearrange("g p t -> p g t"))

        def round_pairs(engine_copy, u, lo, hi):
            engine_copy(
                pairs[:, u, lo:hi].bitcast(BF16).rearrange("p (t i) -> p t i", i=2),
                x_raw[u][:].rearrange("p (i t) -> p t i", i=2)[:, lo:hi],
            )

        def picked(lo, hi):
            return early[:, :, lo - DIRECT : hi - DIRECT] if hi <= MIDDLE else late[:, :, lo - MIDDLE : hi - MIDDLE]

        def gather(u, lo, hi):
            nc.vector.tensor_copy(picked(lo, hi)[:, u, :], pairs[:, u, :].indirect(offs_sb[:, lo // 16 : hi // 16]))

        def woven(lo, hi):
            if hi <= 2 * C:
                return head_x[:, 2 * lo : 2 * hi]
            return (slot_x + [third_x, last_x])[lo // C - 2][:]

        def weave(engine_copy, dst, planes):
            engine_copy(dst.rearrange("p (c u) -> p c u", u=2), planes.rearrange("p u c -> p c u"))

        def quantize(codes, code_scales, woven):
            nc.vector.quantize_mx(out=codes.bitcast(E4M3X4), scales=code_scales, in_=woven.bitcast(BF16))

        def multiply(acc, e, h, codes, code_scales):
            nc.tensor.matmul_mx(
                out=acc,
                lhsT=words[:, e, 2 * P * h : 2 * P * (h + 1)].bitcast(E2M1X4),
                lhsT_scale=scales[:, e, P * h : P * (h + 1)],
                rhs=codes.bitcast(E4M3X4),
                rhs_scale=code_scales,
                start=True,
                stop=True,
            )

        def slots(e):
            return slice(e * C, (e + 1) * C)

        def slot_codes(place):
            return codes_first[:] if place == 0 else codes_rest[:, slots(place - 1)]

        def block(j):
            return slice(j * P, (j + 1) * P)

        def empty(acc, e, h):
            nc.scalar.activation(y[h][:, slots(e)], acc, IDENTITY, bias=bias[:, h, e : e + 1])

        def fetch(dst, h, g, lo, hi):
            nc.vector.tensor_tensor(
                dst[:, lo:hi],
                y[h][:].indirect((pos1_sb, pos2_sb)[g][:, lo // 16 : hi // 16]),
                gates[:, g, lo:hi],
                MULT,
            )

        def turn(dst, src, start, stop):
            nc.tensor.matmul(dst, lhsT=src, rhs=identity[:], is_transpose=True, start=start, stop=stop)

        round_pairs(nc.vector.tensor_copy, 0, 0, CUT)
        round_pairs(nc.scalar.copy, 0, CUT, T)
        nc.vector.tensor_copy(row1[:, 0:T], x_raw[0][:, T : 2 * T])
        round_pairs(nc.gpsimd.tensor_copy, 1, 0, T)
        direct = head_x[:, 0 : 2 * DIRECT].bitcast(BF16).rearrange("p (c d) -> p d c", d=4)
        for d, window in ((0, x_raw[0]), (2, x_raw[1]), (1, row1), (3, row3)):
            nc.scalar.activation(direct[:, d, :], window[:].indirect(offs_sb[:, 0 : DIRECT // 16]), COPY)

        weave(nc.gpsimd.tensor_copy, token_x[:], pairs[:, :, 0:T])
        gather(0, DIRECT, MIDDLE)
        gather(0, MIDDLE, S)
        gather(1, DIRECT, MIDDLE)
        for e in range(MIDDLE // C, E):
            gather(1, e * C, (e + 1) * C)
        weave(nc.gpsimd.tensor_copy, slot_x[0][:, C : 2 * C], picked(MIDDLE - C // 2, MIDDLE))
        weave(nc.scalar.copy, woven(DIRECT, 2 * C), picked(DIRECT, 2 * C))
        weave(nc.scalar.copy, slot_x[0][:, 0:C], picked(2 * C, MIDDLE - C // 2))
        for e in range(MIDDLE // C, E):
            weave(nc.scalar.copy, woven(e * C, (e + 1) * C), picked(e * C, (e + 1) * C))
        for place, e in enumerate(ORDER):
            quantize(slot_codes(place), slot_scales[:, slots(e)], woven(e * C, (e + 1) * C))
            multiply(y0_ps[place][:], e, 0, slot_codes(place), slot_scales[:, slots(e)])
        for place, e in enumerate(ORDER):
            empty(y0_ps[place][:], e, 0)

        ys_turned = bank(5, "ys_turned", T + P)
        ys_long = bank(0, "ys_long", CUT)
        short_first = list(zip(token_codes, PARTS))[::-1]
        for codes, (lo, hi) in short_first:
            quantize(codes[:], token_scales[:, lo:hi], token_x[:, 2 * lo : 2 * hi])

        nc.vector.scalar_tensor_tensor(diagonal[:], gates[:, 1, CUT:T], 1.0, identity[:], MULT, MULT, accum_out=gate_column[:])

        y1_ps = [bank(2 + j, f"y1_ps{j}", 2 * C) for j in range(E // 2)]
        for place, e in enumerate(ORDER):
            multiply(y1_ps[place // 2][:, slots(place % 2)], e, 1, slot_codes(place), slot_scales[:, slots(e)])

        def multiply_turned(acc, h, codes, code_scales):
            nc.tensor.matmul_mx(
                out=acc,
                lhsT=codes.bitcast(E4M3X4),
                lhsT_scale=code_scales,
                rhs=words[:, E, 2 * P * h : 2 * P * (h + 1)].bitcast(E2M1X4),
                rhs_scale=scales[:, E, P * h : P * (h + 1)],
                start=True,
                stop=True,
            )

        multiply_turned(ys_turned[:, T : T + P], 1, token_codes[1][:], token_scales[:, CUT:T])
        for codes, (lo, hi) in short_first:
            for at in range(lo, hi, P):
                multiply_turned(ys_turned[:, at : at + P], 0, codes[:, at - lo : at - lo + P], token_scales[:, at : at + P])
        for place, e in enumerate(ORDER):
            empty(y1_ps[place // 2][:, slots(place % 2)], e, 1)
        multiply(ys_long[:], E, 1, token_codes[0][:], token_scales[:, 0:CUT])

        nc.scalar.activation(plain[:], y[1][:].indirect(pos2_sb[:, CUT // 16 : T // 16]), COPY)
        nc.scalar.copy(base[:], ys_turned[:])
        sums = [bank(number, f"sum{j}", P) for j, number in enumerate((7, 1, 6))]
        back = [bank(number, f"back{j}", P) for j, number in enumerate((2, 3, 5))]
        fetch(first[0], 0, 0, 0, T)
        for j in range(BLOCKS):
            turn(sums[j][:], first[0][:, block(j)], True, False)
        for lo, hi in PARTS:
            fetch(second[0], 0, 1, lo, hi)
        for j in range(BLOCKS):
            turn(sums[j][:], second[0][:, block(j)], False, True)
        for j in range(BLOCKS):
            turn(back[j][:], base[:, block(j)], True, False)
        for j in range(BLOCKS):
            nc.scalar.copy(turned[:, block(j)], sums[j][:])
        across = bank(4, "across", P)
        turn(across[:], plain[:], True, True)
        nc.scalar.activation(gated[:], across[:], COPY, scale=gate_column[:])
        for j in range(BLOCKS):
            turn(back[j][:], turned[:, block(j)], False, True)
        last = bank(6, "last", P)
        turn(last[:], base[:, T : T + P], True, False)
        turn(last[:], gated[:], False, True)
        for lo, hi in PARTS:
            for j in range(lo // P, hi // P):
                nc.scalar.activation(result[0][:, block(j)], back[j][:], IDENTITY, bias=bias[:, 0, E : E + 1])
            nc.scalar.dma_start(out=out[0:P, lo:hi], in_=result[0][:, lo:hi])

        fetch(second[1], 1, 1, 0, CUT)
        fetch(first[1], 1, 0, 0, CUT)
        nc.vector.scalar_tensor_tensor(partial[:, 0:CUT], ys_long[:], bias[:, 1, E : E + 1], second[1][:, 0:CUT], ADD, ADD)
        fetch(first[1], 1, 0, CUT, T)
        nc.vector.tensor_tensor(result[1][:, 0:CUT], partial[:, 0:CUT], first[1][:, 0:CUT], ADD)
        nc.sync.dma_start(out=out[P:N, 0:CUT], in_=result[1][:, 0:CUT])
        nc.vector.scalar_tensor_tensor(result[1][:, CUT:T], last[:], bias[:, 1, E : E + 1], first[1][:, CUT:T], ADD, ADD)
        nc.sync.dma_start(out=out[P:N, CUT:T], in_=result[1][:, CUT:T])
